import numpy as np
import ml_dtypes


def mxq(x, axis, fmt="e4m3"):
    dtype, down = {"e4m3": (ml_dtypes.float8_e4m3fn, 7), "e5m2": (ml_dtypes.float8_e5m2, 14)}[fmt]
    v = np.moveaxis(np.asarray(x, np.float32).astype(ml_dtypes.bfloat16).astype(np.float64), axis, -1)
    blocks = v.reshape(v.shape[:-1] + (-1, 32))
    amax = np.abs(blocks).max(-1, keepdims=True)
    byte = np.maximum(np.where(amax > 0, np.frexp(amax)[1] - 1 + 127, 0) - down, 1)
    scale = np.exp2(byte - 127.0)
    codes = (blocks / scale).astype(np.float32).astype(dtype).astype(np.float64)
    return np.moveaxis((codes * scale).reshape(v.shape), -1, axis)


WIDE = False


def mx_kscale(k):
    if not WIDE:
        return np.ones(k)
    levels = np.array([10, -10, 5, -5, 0])
    if k % 512:
        return np.exp2(np.random.permutation(np.resize(levels, k // 32))).repeat(32)
    a = np.empty((k // 512, 16))
    for p in range(k // 512):
        a[p, :8] = np.random.permutation(np.resize(levels, 8))
        for g in range(8):
            far = levels[np.abs(levels - a[p, g]) >= 10]
            a[p, g + 8] = far[np.random.randint(len(far))]
    return np.exp2(a.ravel()).repeat(32)


BF16 = ml_dtypes.bfloat16


def bf(x):
    return np.asarray(x, np.float32).astype(BF16)


def f64(x):
    return np.asarray(x).astype(np.float64)


E2M1 = np.array([0.0, 0.5, 1.0, 1.5, 2.0, 3.0, 4.0, 6.0, -0.0, -0.5, -1.0, -1.5, -2.0, -3.0, -4.0, -6.0])


def pack_weight(w, fmt):
    k, n = w.shape
    w = f64(bf(w)).reshape(k // 32, 32, n)
    amax = np.abs(w).max(1)
    if fmt == "e4m3":
        byte = np.frexp(amax)[1] - 1 + 127 - 7
    else:
        mant, ex = np.frexp(amax / 6.0)
        byte = np.where(mant > 0.5, ex, ex - 1) + 127
    byte = np.clip(np.where(amax > 0, byte, 1), 1, 254)
    scaled = (w * np.exp2(127.0 - byte)[:, None, :]).reshape(k, n).astype(np.float32)
    by_word = np.ascontiguousarray(scaled.reshape(k // 512, 128, 4, n).transpose(0, 1, 3, 2))
    if fmt == "e4m3":
        words = by_word.astype(ml_dtypes.float8_e4m3fn).view(np.uint8)
    else:
        c = by_word.astype(ml_dtypes.float4_e2m1fn).view(np.uint8) & 0xF
        words = c[..., 0::2] | (c[..., 1::2] << 4)
    return np.ascontiguousarray(words), np.ascontiguousarray(byte.astype(np.uint8).reshape(k // 512, 16, n))


def unpack_weight(words, scales, fmt):
    g, p, n, _ = words.shape
    if fmt == "e4m3":
        vals = np.ascontiguousarray(words).view(ml_dtypes.float8_e4m3fn).astype(np.float64)
    else:
        nib = np.empty((g, p, n, 4), np.uint8)
        nib[..., 0::2] = words & 0xF
        nib[..., 1::2] = words >> 4
        vals = E2M1[nib]
    vals = vals * np.repeat(np.exp2(scales.astype(np.float64) - 127.0), 8, axis=1)[..., None]
    return vals.transpose(0, 1, 3, 2).reshape(g * 512, n)
def pack4(w):
    words, scales = pack_weight(w, "e2m1")
    return words.reshape(words.shape[0], 128, -1), scales


def unpack4(words, scales):
    return unpack_weight(words.reshape(words.shape[0], 128, -1, 2), scales, "e2m1")


E4M3FN = np.array([(-1.0 if i & 128 else 1.0) * ((1.0 + (i & 7) / 8.0) * 2.0 ** (((i >> 3) & 15) - 7) if i & 120 else (i & 7) * 2.0 ** -9) for i in range(256)])


def e4m3fn_bytes(y):
    return np.clip(np.asarray(y, np.float64), -448.0, 448.0).astype(np.float32).astype(ml_dtypes.float8_e4m3fn).view(np.uint8)


def e4m3fn_values(b):
    return E4M3FN[b]


B, P, K, D, N, G = 2, 256, 3072, 1024, 3072, 128

FP8_MAX = 448.0


def setup_inputs():
    s, t = mx_kscale(K), mx_kscale(D)
    x = np.random.standard_normal((B * P, K)) * s
    w = np.random.standard_normal((K, D)) / np.sqrt(K) / s[:, None]
    x_scale = (np.abs(x).reshape(B * P, K // G, G).max(axis=2) / FP8_MAX).astype(np.float32)
    w_scale = (np.abs(w).reshape(K // G, G, D // G, G).max(axis=(1, 3)) / FP8_MAX).astype(np.float32)
    x_bytes = e4m3fn_bytes(x / np.repeat(f64(x_scale), G, axis=1))
    w_bytes = e4m3fn_bytes(w / np.repeat(np.repeat(f64(w_scale), G, axis=0), G, axis=1))
    v_words, v_scales = pack4(np.random.standard_normal((D, N)) / np.sqrt(D) / t[:, None])
    return {"x_bytes": x_bytes, "x_scale": x_scale,
            "w_bytes": w_bytes, "w_scale": w_scale,
            "gain": bf((1 + 0.1 * np.random.standard_normal(D)) * t),
            "pos": bf(0.5 * np.random.standard_normal((P, D)) * t),
            "v_words": v_words, "v_scales": v_scales,
            "bias": bf(0.3 * np.random.standard_normal(N))}


def reference(x_bytes, x_scale, w_bytes, w_scale, gain, pos, v_words, v_scales, bias):
    x = e4m3fn_values(x_bytes) * np.repeat(f64(x_scale), G, axis=1)
    w = e4m3fn_values(w_bytes) * np.repeat(np.repeat(f64(w_scale), G, axis=0), G, axis=1)
    e = mxq(x, 1, "e4m3") @ mxq(w, 0, "e4m3")
    h = (e * f64(gain)).reshape(B, P, D) + f64(pos)
    h = h.reshape(B * P, D)
    y = mxq(h, 1, "e4m3") @ unpack4(v_words, v_scales)
    return y + f64(bias)

@@ -1,0 +1,295 @@
+from contextlib import ExitStack
+
+import concourse.mybir as mybir
+from concourse.masks import make_identity
+
+F32 = mybir.dt.float32
+BF16 = mybir.dt.bfloat16
+I32 = mybir.dt.int32
+U32 = mybir.dt.uint32
+U8 = mybir.dt.uint8
+FP8 = mybir.dt.float8_e4m3fn
+FP8X4 = mybir.dt.float8_e4m3fn_x4
+FP4X4 = mybir.dt.float4_e2m1fn_x4
+MULT = mybir.AluOpType.mult
+ADD = mybir.AluOpType.add
+COPY = mybir.ActivationFunctionType.Copy
+
+P = 128
+PASS = 512
+TOK, K, D, N = 512, 3072, 1024, 3072
+IMAGE = 256
+PASSES = K // PASS
+UNITS = 2 * PASSES
+TOKEN_TILES = TOK // P
+COLUMN_BLOCKS = N // 512
+FLOPS = 2 * TOK * K * D + 2 * TOK * D * N
+
+VECTOR_WIDENS = (PASSES,)
+SCALAR_SCALES = (UNITS - 1,)
+WIDEN_IN_STEP = (1, 2, 1, 2, 1, 1, 1, 1, 0, 0, 0, 0)
+STORES = ((1, 1, 2, 2), (2, 2, 2), (2, 2, 2), (2, 2, 1, 1))
+
+
+def tile_patch_embed_qkv_d4_kernel(tc, x_bytes, x_scale, w_bytes, w_scale, gain, pos, v_words, v_scales, bias, out):
+    nc = tc.nc
+    with ExitStack() as ctx:
+        keep = ctx.enter_context(tc.tile_pool(name="keep", bufs=1))
+        stage = ctx.enter_context(tc.tile_pool(name="stage", bufs=3))
+        wide = ctx.enter_context(tc.tile_pool(name="wide", bufs=6))
+        outs = ctx.enter_context(tc.tile_pool(name="outs", bufs=5))
+        psum = ctx.enter_context(tc.psum_pool(name="psum", bufs=1))
+        ctx.enter_context(tc.manual_schedule())
+
+        def bank(b, dtype=F32):
+            return psum.tile([P, 512 if dtype == F32 else 1024], dtype, name="bank%d" % b)
+
+        ident = keep.tile([P, P], F32, name="ident")
+        make_identity(nc, ident[:])
+        ident_b = keep.tile([P, P], BF16, name="ident_b")
+
+        xs = keep.tile([P, TOKEN_TILES * 24], F32, name="xs")
+        nc.scalar.dma_start(out=xs[:].rearrange("p (i c) -> p i c", i=TOKEN_TILES), in_=x_scale.rearrange("(i p) c -> p i c", p=P))
+        w_scale_all = keep.tile([P, 192], F32, name="w_scale_all")
+        nc.scalar.dma_start(out=w_scale_all[:], in_=w_scale.rearrange("c d -> (c d)").partition_broadcast(P))
+
+        xb = [keep.tile([P, 2048], U8, name="xb%d" % g) for g in range(PASSES)]
+        wb = [keep.tile([P, 2048], U8, name="wb%d" % u) for u in range(UNITS)]
+
+        def load_x(g, tiles=slice(0, 4)):
+            nc.sync.dma_start(
+                out=xb[g][:].rearrange("p (i k) -> p i k", i=4)[:, tiles],
+                in_=x_bytes.rearrange("(i p) k -> p i k", p=P)[:, tiles, PASS * g:PASS * g + PASS])
+
+        def load_w(u, rows=slice(0, 4)):
+            half, g = divmod(u, PASSES)
+            nc.sync.dma_start(
+                out=wb[u][:].rearrange("p (t n) -> p t n", t=4)[:, rows],
+                in_=w_bytes[PASS * g:PASS * g + PASS, 512 * half:512 * half + 512].rearrange("(p t) n -> p t n", t=4)[:, rows])
+
+        for part in (slice(0, 2), slice(2, 4)):
+            load_x(0, part)
+            load_w(0, part)
+        for g in range(1, PASSES):
+            load_x(g)
+            load_w(g)
+        pos_sb = keep.tile([P, 2 * D], BF16, name="pos_sb")
+        nc.sync.dma_start(out=pos_sb[:].rearrange("p (i j) -> p i j", i=2), in_=pos.rearrange("(i p) j -> p i j", p=P))
+        gain_b = keep.tile([P, 8], BF16, name="gain_b")
+        nc.sync.dma_start(out=gain_b[:].rearrange("p (h t) -> p h t", h=2), in_=gain.rearrange("(h p t) -> p h t", h=2, t=4))
+        for u in range(PASSES, UNITS):
+            load_w(u)
+        vw = [keep.tile([P, 2 * N], U8, name="vw%d" % h, align_bytes=64) for h in range(2)]
+        for h in range(2):
+            nc.sync.dma_start(out=vw[h][:].bitcast(I32), in_=v_words[h].bitcast(I32))
+        vs = keep.tile([P, 2 * N], U8, name="vs", align_bytes=64)
+        nc.gpsimd.memset(vs[:].bitcast(I32), 0)
+        for q in range(4):
+            nc.sync.dma_start(
+                out=vs[32 * q:32 * q + 4, :].rearrange("p (h n) -> p h n", h=2).bitcast(I32),
+                in_=v_scales[:, 4 * q:4 * q + 4, :].rearrange("h r n -> r h n").bitcast(I32))
+        bias_sb = keep.tile([P, N], BF16, name="bias_sb")
+        nc.sync.dma_start(out=bias_sb[:], in_=bias.partition_broadcast(P))
+
+        wsc = keep.tile([P, 8 * PASSES], F32, name="wsc")
+        gain_f = keep.tile([P, 8], F32, name="gain_f")
+
+        def pick_w_scales():
+            for q in range(4):
+                rows = slice(32 * q, 32 * q + 32)
+                nc.scalar.copy(
+                    out=wsc[rows, :].rearrange("p (g d) -> p g d", d=8),
+                    in_=w_scale_all[rows, :].rearrange("p (g q d) -> p q g d", q=4, d=8)[:, q])
+
+        xw, xint, xq, xqs, xbank = {}, {}, {}, {}, {}
+
+        def x_widen(g):
+            xw[g] = stage.tile([P, 2048], BF16, name="xw")
+            for i in range(TOKEN_TILES):
+                for c in range(4):
+                    cols = slice(512 * i + 128 * c, 512 * i + 128 * c + 128)
+                    col = 24 * i + 4 * g + c
+                    nc.vector.tensor_scalar(
+                        out=xw[g][:, cols], in0=xb[g][:, cols].bitcast(FP8), scalar1=xs[:, col:col + 1], scalar2=None, op0=MULT)
+
+        def x_turn(g):
+            words = xw[g][:].bitcast(F32)
+            for b in range(2):
+                xbank[g, b] = bank(4 + (2 * g + b) % 4)
+                for i in range(2):
+                    for u in range(2):
+                        first = 256 * (2 * b + i) + u
+                        at = 128 * (2 * i + u)
+                        nc.tensor.transpose(xbank[g, b][:, at:at + 128], words[:, first:first + 255:2], ident[:])
+
+        def x_out(g):
+            xint[g] = stage.tile([P, 2048], BF16, name="xint", align_bytes=64)
+            for b in range(2):
+                nc.scalar.copy(
+                    out=xint[g][:, 1024 * b:1024 * b + 1024].bitcast(F32).rearrange("p (i r u) -> p i r u", i=2, u=2),
+                    in_=xbank[g, b][:].rearrange("p (i u r) -> p i r u", i=2, u=2))
+
+        def x_quant(g):
+            xq[g] = keep.tile([P, TOK], U32, name="xq%d" % g, align_bytes=64)
+            xqs[g] = keep.tile([P, TOK], U8, name="xqs%d" % g, align_bytes=64)
+            nc.vector.quantize_mx(out=xq[g][:].bitcast(FP8X4), scales=xqs[g][:], in_=xint[g][:])
+
+        ww, wint, wq, wqs = {}, {}, {}, {}
+
+        def w_widen(u):
+            ww[u] = wide.tile([P, 2048], BF16, name="ww")
+            parts = 2 if u == 0 else 1
+            for j in range(parts):
+                cols = slice(2048 // parts * j, 2048 // parts * (j + 1))
+                if u in VECTOR_WIDENS:
+                    nc.vector.tensor_copy(out=ww[u][:, cols], in_=wb[u][:, cols].bitcast(FP8))
+                else:
+                    nc.scalar.copy(out=ww[u][:, cols], in_=wb[u][:, cols].bitcast(FP8))
+
+        def w_scale_in(u):
+            half, g = divmod(u, PASSES)
+            wint[u] = stage.tile([P, 2048], BF16, name="wint", align_bytes=64)
+            src = ww[u][:].rearrange("p (j b m t) -> p b m t j", j=4, b=4, t=4)
+            dst = wint[u][:].rearrange("p (t b m j) -> p b m t j", t=4, b=4, j=4)
+            for b in range(4):
+                col = 8 * g + 4 * half + b
+                if u in SCALAR_SCALES:
+                    nc.scalar.activation(out=dst[:, b], in_=src[:, b], func=COPY, scale=wsc[:, col:col + 1])
+                else:
+                    nc.vector.tensor_scalar(out=dst[:, b], in0=src[:, b], scalar1=wsc[:, col:col + 1], scalar2=None, op0=MULT)
+
+        def w_quant(u):
+            wq[u] = stage.tile([P, 512], U32, name="wq", align_bytes=64)
+            wqs[u] = stage.tile([P, 512], U8, name="wqs", align_bytes=64)
+            nc.vector.quantize_mx(out=wq[u][:].bitcast(FP8X4), scales=wqs[u][:], in_=wint[u][:])
+
+        e = {}
+
+        def product_1(u):
+            half, g = divmod(u, PASSES)
+            for t in range(4):
+                if g == 0:
+                    e[half, t] = bank(4 * half + t)
+                cols = slice(128 * t, 128 * t + 128)
+                nc.tensor.matmul_mx(
+                    out=e[half, t][:],
+                    lhsT=wq[u][:, cols].bitcast(FP8X4), lhsT_scale=wqs[u][:, cols],
+                    rhs=xq[g][:].bitcast(FP8X4), rhs_scale=xqs[g][:], start=(g == 0), stop=(g == PASSES - 1))
+
+        pos_t = keep.tile([P, 2048], BF16, name="pos_t")
+
+        def pos_turn(half):
+            pb = bank(6 + half, BF16)
+            for t in range(4):
+                for i in range(2):
+                    first = D * i + 512 * half + t
+                    at = IMAGE * t + 128 * i
+                    nc.tensor.transpose(pb[:, at:at + 128], pos_sb[:, first:first + 509:4], ident_b[:])
+            nc.scalar.copy(out=pos_t[:, 1024 * half:1024 * half + 1024], in_=pb[:])
+
+        hs = [keep.tile([P, 4 * TOK], BF16, name="hs%d" % h) for h in range(2)]
+        hint = [keep.tile([P, 4 * TOK], BF16, name="hint%d" % h, align_bytes=64) for h in range(2)]
+        hq = [keep.tile([P, TOK], U32, name="hq%d" % h, align_bytes=64) for h in range(2)]
+        hqs = [keep.tile([P, TOK], U8, name="hqs%d" % h, align_bytes=64) for h in range(2)]
+
+        def h_add(half, lo, hi, slices=range(4)):
+            r = lo % IMAGE
+            for t in slices:
+                at = 1024 * half + IMAGE * t + r
+                nc.vector.scalar_tensor_tensor(
+                    out=hs[half][:, TOK * t + lo:TOK * t + hi], in0=e[half, t][:, lo:hi],
+                    scalar=gain_f[:, 4 * half + t:4 * half + t + 1], in1=pos_t[:, at:at + hi - lo], op0=MULT, op1=ADD)
+
+        def h_weave(half, i, n=1):
+            nc.scalar.copy(
+                out=hint[half][:, 512 * i:512 * (i + n)].rearrange("p (r t) -> p r t", t=4),
+                in_=hs[half][:].rearrange("p (t r) -> p r t", t=4)[:, 128 * i:128 * (i + n)])
+
+        def h_quant(half, i, n=1):
+            toks = slice(128 * i, 128 * (i + n))
+            nc.vector.quantize_mx(
+                out=hq[half][:, toks].bitcast(FP8X4), scales=hqs[half][:, toks], in_=hint[half][:, 512 * i:512 * (i + n)])
+
+        ob, ot = {}, {}
+
+        def product_2(n):
+            i, c = divmod(n, COLUMN_BLOCKS)
+            ob[n] = bank(n % 8)
+            toks = slice(128 * i, 128 * i + 128)
+            for h in range(2):
+                nc.tensor.matmul_mx(
+                    out=ob[n][:],
+                    lhsT=hq[h][:, toks].bitcast(FP8X4), lhsT_scale=hqs[h][:, toks],
+                    rhs=vw[h][:, 1024 * c:1024 * c + 1024].bitcast(FP4X4), rhs_scale=vs[:, N * h + 512 * c:N * h + 512 * c + 512],
+                    start=(h == 0), stop=(h == 1))
+
+        def finish(n):
+            i, c = divmod(n, COLUMN_BLOCKS)
+            first, width = 0, STORES[i][0]
+            for k in range(1, len(STORES[i])):
+                if sum(STORES[i][:k]) <= c:
+                    first, width = sum(STORES[i][:k]), STORES[i][k]
+            if c == first:
+                ot[i, first] = outs.tile([P, 1024], F32, name="ot")
+            o = ot[i, first]
+            at = 512 * (c - first)
+            nc.vector.tensor_tensor(out=o[:, at:at + 512], in0=ob[n][:], in1=bias_sb[:, 512 * c:512 * c + 512], op=ADD)
+            if c == first + width - 1:
+                nc.sync.dma_start(out=out[128 * i:128 * i + 128, 512 * first:512 * (c + 1)], in_=o[:, 0:512 * width])
+
+        nc.scalar.activation(out=ident_b[:], in_=ident[:], func=COPY)
+        to_widen = list(range(UNITS))
+        for g in range(2):
+            x_widen(g)
+            x_turn(g)
+            w_widen(to_widen.pop(0))
+            if g == 0:
+                pick_w_scales()
+            x_out(g)
+        w_scale_in(0)
+        for s in range(UNITS):
+            for j in range(WIDEN_IN_STEP[s]):
+                w_widen(to_widen.pop(0))
+            if s + 2 < PASSES:
+                x_widen(s + 2)
+                x_turn(s + 2)
+                x_out(s + 2)
+            if s == 4:
+                nc.scalar.copy(out=gain_f[:], in_=gain_b[:])
+                pos_turn(0)
+                pos_turn(1)
+            if s == UNITS - 2:
+                w_quant(s)
+            if s + 1 < UNITS:
+                w_scale_in(s + 1)
+            if s < PASSES:
+                x_quant(s)
+            if s == UNITS - 1:
+                h_add(0, 0, IMAGE)
+                h_weave(0, 0, 2)
+            if s != UNITS - 2:
+                w_quant(s)
+            product_1(s)
+
+        h_add(0, IMAGE, TOK)
+        h_add(1, 0, 128)
+        h_weave(1, 0)
+        h_add(1, 128, IMAGE)
+        h_weave(1, 1)
+        h_quant(0, 0, 2)
+        h_quant(1, 0)
+        h_add(1, IMAGE, TOK, range(0, 2))
+        for n in range(4):
+            product_2(n)
+        for n in range(TOKEN_TILES * COLUMN_BLOCKS):
+            finish(n)
+            if n == 0:
+                h_add(1, IMAGE, TOK, range(2, 4))
+                h_quant(1, 1)
+                h_weave(0, 2, 2)
+                h_weave(1, 2, 2)
+            if n == 7:
+                h_quant(0, 2, 2)
+                h_quant(1, 2, 2)
+            if n + 4 < TOKEN_TILES * COLUMN_BLOCKS:
+                product_2(n + 4)

@@ -25,9 +25,9 @@ TOKEN_TILES = TOK // P
 COLUMN_BLOCKS = N // 512
 FLOPS = 2 * TOK * K * D + 2 * TOK * D * N
 
-VECTOR_WIDENS = (PASSES,)
+VECTOR_WIDENS = ()
 SCALAR_SCALES = (UNITS - 1,)
-WIDEN_IN_STEP = (1, 2, 1, 2, 1, 1, 1, 1, 0, 0, 0, 0)
+WIDEN_IN_STEP = (1, 1, 1, 1, 2, 2, 1, 1, 0, 0, 0, 0)
 STORES = ((1, 1, 2, 2), (2, 2, 2), (2, 2, 2), (2, 2, 1, 1))
 
 
@@ -109,8 +109,11 @@ def tile_patch_embed_qkv_d4_kernel(tc, x_bytes, x_scale, w_bytes, w_scale, gain,
                 for c in range(4):
                     cols = slice(512 * i + 128 * c, 512 * i + 128 * c + 128)
                     col = 24 * i + 4 * g + c
-                    nc.vector.tensor_scalar(
-                        out=xw[g][:, cols], in0=xb[g][:, cols].bitcast(FP8), scalar1=xs[:, col:col + 1], scalar2=None, op0=MULT)
+                    if g >= 2 and i >= 2:
+                        nc.scalar.activation(out=xw[g][:, cols], in_=xb[g][:, cols].bitcast(FP8), func=COPY, scale=xs[:, col:col + 1])
+                    else:
+                        nc.vector.tensor_scalar(
+                            out=xw[g][:, cols], in0=xb[g][:, cols].bitcast(FP8), scalar1=xs[:, col:col + 1], scalar2=None, op0=MULT)
 
         def x_turn(g):
             words = xw[g][:].bitcast(F32)
@@ -248,11 +251,12 @@ def tile_patch_embed_qkv_d4_kernel(tc, x_bytes, x_scale, w_bytes, w_scale, gain,
             x_out(g)
         w_scale_in(0)
         for s in range(UNITS):
-            for j in range(WIDEN_IN_STEP[s]):
-                w_widen(to_widen.pop(0))
             if s + 2 < PASSES:
                 x_widen(s + 2)
                 x_turn(s + 2)
+            for j in range(WIDEN_IN_STEP[s]):
+                w_widen(to_widen.pop(0))
+            if s + 2 < PASSES:
                 x_out(s + 2)
             if s == 4:
                 nc.scalar.copy(out=gain_f[:], in_=gain_b[:])

@@ -152,8 +152,8 @@ def tile_patch_embed_qkv_d4_kernel(tc, x_bytes, x_scale, w_bytes, w_scale, gain,
         def w_scale_in(u):
             half, g = divmod(u, PASSES)
             wint[u] = stage.tile([P, 2048], BF16, name="wint", align_bytes=64)
-            src = ww[u][:].rearrange("p (j b m t) -> p b m t j", j=4, b=4, t=4)
-            dst = wint[u][:].rearrange("p (t b m j) -> p b m t j", t=4, b=4, j=4)
+            src = ww[u][:].rearrange("p (j b m t) -> p b m j t", j=4, b=4, t=4)
+            dst = wint[u][:].rearrange("p (t b m j) -> p b m j t", t=4, b=4, j=4)
             for b in range(4):
                 col = 8 * g + 4 * half + b
                 if u in SCALAR_SCALES:
@@ -205,8 +205,8 @@ def tile_patch_embed_qkv_d4_kernel(tc, x_bytes, x_scale, w_bytes, w_scale, gain,
 
         def h_weave(half, i, n=1):
             nc.scalar.copy(
-                out=hint[half][:, 512 * i:512 * (i + n)].rearrange("p (r t) -> p r t", t=4),
-                in_=hs[half][:].rearrange("p (t r) -> p r t", t=4)[:, 128 * i:128 * (i + n)])
+                out=hint[half][:, 512 * i:512 * (i + n)].rearrange("p (c r t) -> p c t r", r=4, t=4),
+                in_=hs[half][:].rearrange("p (t c r) -> p c t r", t=4, r=4)[:, 32 * i:32 * (i + n)])
 
         def h_quant(half, i, n=1):
             toks = slice(128 * i, 128 * (i + n))

@@ -25,9 +25,9 @@ TOKEN_TILES = TOK // P
 COLUMN_BLOCKS = N // 512
 FLOPS = 2 * TOK * K * D + 2 * TOK * D * N
 
-VECTOR_WIDENS = ()
-SCALAR_SCALES = (UNITS - 1,)
-WIDEN_IN_STEP = (1, 1, 1, 1, 2, 2, 1, 1, 0, 0, 0, 0)
+SCALAR_BLOCKS = 14
+BLOCKS_IN_STEP = (0, 0, 0, 0, 3, 3)
+OUT_BUFS = 5
 STORES = ((1, 1, 2, 2), (2, 2, 2), (2, 2, 2), (2, 2, 1, 1))
 
 
@@ -36,8 +36,7 @@ def tile_patch_embed_qkv_d4_kernel(tc, x_bytes, x_scale, w_bytes, w_scale, gain,
     with ExitStack() as ctx:
         keep = ctx.enter_context(tc.tile_pool(name="keep", bufs=1))
         stage = ctx.enter_context(tc.tile_pool(name="stage", bufs=3))
-        wide = ctx.enter_context(tc.tile_pool(name="wide", bufs=6))
-        outs = ctx.enter_context(tc.tile_pool(name="outs", bufs=5))
+        outs = ctx.enter_context(tc.tile_pool(name="outs", bufs=OUT_BUFS))
         psum = ctx.enter_context(tc.psum_pool(name="psum", bufs=1))
         ctx.enter_context(tc.manual_schedule())
 
@@ -49,36 +48,36 @@ def tile_patch_embed_qkv_d4_kernel(tc, x_bytes, x_scale, w_bytes, w_scale, gain,
         ident_b = keep.tile([P, P], BF16, name="ident_b")
 
         xs = keep.tile([P, TOKEN_TILES * 24], F32, name="xs")
-        nc.scalar.dma_start(out=xs[:].rearrange("p (i c) -> p i c", i=TOKEN_TILES), in_=x_scale.rearrange("(i p) c -> p i c", p=P))
+        nc.scalar.dma_start(out=xs[:].rearrange("p (a c) -> p a c", a=2), in_=x_scale.rearrange("(a p i) c -> p a (i c)", a=2, i=2))
+
+        xb = {(a, j): keep.tile([P, 2048], U8, name="xb%d%d" % (a, j)) for a in range(2) for j in range(PASSES // 2)}
+        wb = [keep.tile([P, 4096], U8, name="wb%d" % g) for g in range(PASSES)]
+
+        def load_x(a, j):
+            nc.sync.dma_start(
+                out=xb[a, j][:].rearrange("p (i k) -> p i k", i=2),
+                in_=x_bytes.rearrange("(a p i) k -> a p i k", a=2, i=2)[a, :, :, 1024 * j:1024 * j + 1024])
+
+        def load_w(g, cols=slice(0, 4096)):
+            nc.sync.dma_start(out=wb[g][:, cols], in_=w_bytes[PASS * g:PASS * g + PASS, :].rearrange("(p t) n -> p (t n)", t=4)[:, cols])
+
+        load_x(0, 0)
+        load_w(0, slice(0, 2048))
+        load_x(1, 0)
+        load_w(0, slice(2048, 4096))
         w_scale_all = keep.tile([P, 192], F32, name="w_scale_all")
-        nc.scalar.dma_start(out=w_scale_all[:], in_=w_scale.rearrange("c d -> (c d)").partition_broadcast(P))
-
-        xb = [keep.tile([P, 2048], U8, name="xb%d" % g) for g in range(PASSES)]
-        wb = [keep.tile([P, 2048], U8, name="wb%d" % u) for u in range(UNITS)]
-
-        def load_x(g, tiles=slice(0, 4)):
-            nc.sync.dma_start(
-                out=xb[g][:].rearrange("p (i k) -> p i k", i=4)[:, tiles],
-                in_=x_bytes.rearrange("(i p) k -> p i k", p=P)[:, tiles, PASS * g:PASS * g + PASS])
-
-        def load_w(u, rows=slice(0, 4)):
-            half, g = divmod(u, PASSES)
-            nc.sync.dma_start(
-                out=wb[u][:].rearrange("p (t n) -> p t n", t=4)[:, rows],
-                in_=w_bytes[PASS * g:PASS * g + PASS, 512 * half:512 * half + 512].rearrange("(p t) n -> p t n", t=4)[:, rows])
-
-        for part in (slice(0, 2), slice(2, 4)):
-            load_x(0, part)
-            load_w(0, part)
-        for g in range(1, PASSES):
-            load_x(g)
-            load_w(g)
+        nc.sync.dma_start(out=w_scale_all[:], in_=w_scale.rearrange("c d -> (c d)").partition_broadcast(P))
         pos_sb = keep.tile([P, 2 * D], BF16, name="pos_sb")
-        nc.sync.dma_start(out=pos_sb[:].rearrange("p (i j) -> p i j", i=2), in_=pos.rearrange("(i p) j -> p i j", p=P))
+        for g in range(1, PASSES):
+            if g % 2 == 1 and g + 1 < PASSES:
+                load_x(0, (g + 1) // 2)
+            load_w(g)
+            if g % 2 == 1 and g + 1 < PASSES:
+                load_x(1, (g + 1) // 2)
+            if g == 1:
+                nc.sync.dma_start(out=pos_sb[:], in_=pos.rearrange("(p i) j -> p (i j)", i=2))
         gain_b = keep.tile([P, 8], BF16, name="gain_b")
         nc.sync.dma_start(out=gain_b[:].rearrange("p (h t) -> p h t", h=2), in_=gain.rearrange("(h p t) -> p h t", h=2, t=4))
-        for u in range(PASSES, UNITS):
-            load_w(u)
         vw = [keep.tile([P, 2 * N], U8, name="vw%d" % h, align_bytes=64) for h in range(2)]
         for h in range(2):
             nc.sync.dma_start(out=vw[h][:].bitcast(I32), in_=v_words[h].bitcast(I32))
@@ -103,34 +102,33 @@ def tile_patch_embed_qkv_d4_kernel(tc, x_bytes, x_scale, w_bytes, w_scale, gain,
 
         xw, xint, xq, xqs, xbank = {}, {}, {}, {}, {}
 
-        def x_widen(g):
-            xw[g] = stage.tile([P, 2048], BF16, name="xw")
-            for i in range(TOKEN_TILES):
+        def x_widen(g, a):
+            if a == 0:
+                xw[g] = stage.tile([P, 2048], BF16, name="xw")
+            for i in range(2):
                 for c in range(4):
-                    cols = slice(512 * i + 128 * c, 512 * i + 128 * c + 128)
-                    col = 24 * i + 4 * g + c
-                    if g >= 2 and i >= 2:
-                        nc.scalar.activation(out=xw[g][:, cols], in_=xb[g][:, cols].bitcast(FP8), func=COPY, scale=xs[:, col:col + 1])
-                    else:
-                        nc.vector.tensor_scalar(
-                            out=xw[g][:, cols], in0=xb[g][:, cols].bitcast(FP8), scalar1=xs[:, col:col + 1], scalar2=None, op0=MULT)
+                    at = 1024 * a + 512 * i + 128 * c
+                    src = 1024 * i + 512 * (g % 2) + 128 * c
+                    col = 24 * (2 * a + i) + 4 * g + c
+                    nc.vector.tensor_scalar(
+                        out=xw[g][:, at:at + 128], in0=xb[a, g // 2][:, src:src + 128].bitcast(FP8),
+                        scalar1=xs[:, col:col + 1], scalar2=None, op0=MULT)
 
-        def x_turn(g):
+        def x_turn(g, a):
             words = xw[g][:].bitcast(F32)
-            for b in range(2):
-                xbank[g, b] = bank(4 + (2 * g + b) % 4)
-                for i in range(2):
-                    for u in range(2):
-                        first = 256 * (2 * b + i) + u
-                        at = 128 * (2 * i + u)
-                        nc.tensor.transpose(xbank[g, b][:, at:at + 128], words[:, first:first + 255:2], ident[:])
+            xbank[g, a] = bank(4 + (2 * g + a) % 4)
+            for i in range(2):
+                for u in range(2):
+                    first = 256 * (2 * a + i) + u
+                    at = 128 * (2 * i + u)
+                    nc.tensor.transpose(xbank[g, a][:, at:at + 128], words[:, first:first + 255:2], ident[:])
 
-        def x_out(g):
-            xint[g] = stage.tile([P, 2048], BF16, name="xint", align_bytes=64)
-            for b in range(2):
-                nc.scalar.copy(
-                    out=xint[g][:, 1024 * b:1024 * b + 1024].bitcast(F32).rearrange("p (i r u) -> p i r u", i=2, u=2),
-                    in_=xbank[g, b][:].rearrange("p (i u r) -> p i r u", i=2, u=2))
+        def x_out(g, a):
+            if a == 0:
+                xint[g] = stage.tile([P, 2048], BF16, name="xint", align_bytes=64)
+            nc.scalar.copy(
+                out=xint[g][:, 1024 * a:1024 * a + 1024].bitcast(F32).rearrange("p (i r u) -> p i r u", i=2, u=2),
+                in_=xbank[g, a][:].rearrange("p (i u r) -> p i r u", i=2, u=2))
 
         def x_quant(g):
             xq[g] = keep.tile([P, TOK], U32, name="xq%d" % g, align_bytes=64)
@@ -139,27 +137,22 @@ def tile_patch_embed_qkv_d4_kernel(tc, x_bytes, x_scale, w_bytes, w_scale, gain,
 
         ww, wint, wq, wqs = {}, {}, {}, {}
 
-        def w_widen(u):
-            ww[u] = wide.tile([P, 2048], BF16, name="ww")
-            parts = 2 if u == 0 else 1
-            for j in range(parts):
-                cols = slice(2048 // parts * j, 2048 // parts * (j + 1))
-                if u in VECTOR_WIDENS:
-                    nc.vector.tensor_copy(out=ww[u][:, cols], in_=wb[u][:, cols].bitcast(FP8))
-                else:
-                    nc.scalar.copy(out=ww[u][:, cols], in_=wb[u][:, cols].bitcast(FP8))
+        def w_widen(g, cols=slice(0, 4096)):
+            if cols.start == 0:
+                ww[g] = keep.tile([P, 4096], BF16, name="ww%d" % g)
+            nc.scalar.copy(out=ww[g][:, cols], in_=wb[g][:, cols].bitcast(FP8))
 
-        def w_scale_in(u):
+        def w_weave(u, b, on_scalar):
             half, g = divmod(u, PASSES)
-            wint[u] = stage.tile([P, 2048], BF16, name="wint", align_bytes=64)
-            src = ww[u][:].rearrange("p (j b m t) -> p b m j t", j=4, b=4, t=4)
-            dst = wint[u][:].rearrange("p (t b m j) -> p b m j t", t=4, b=4, j=4)
-            for b in range(4):
-                col = 8 * g + 4 * half + b
-                if u in SCALAR_SCALES:
-                    nc.scalar.activation(out=dst[:, b], in_=src[:, b], func=COPY, scale=wsc[:, col:col + 1])
-                else:
-                    nc.vector.tensor_scalar(out=dst[:, b], in0=src[:, b], scalar1=wsc[:, col:col + 1], scalar2=None, op0=MULT)
+            if u not in wint:
+                wint[u] = stage.tile([P, 2048], BF16, name="wint_s" if on_scalar else "wint_v", align_bytes=64)
+            src = ww[g][:].rearrange("p (j b m t) -> p b m j t", j=4, b=8, t=4)[:, 4 * half + b]
+            dst = wint[u][:].rearrange("p (t b m j) -> p b m j t", t=4, b=4, j=4)[:, b]
+            col = 8 * g + 4 * half + b
+            if on_scalar:
+                nc.scalar.activation(out=dst, in_=src, func=COPY, scale=wsc[:, col:col + 1])
+            else:
+                nc.vector.tensor_scalar(out=dst, in0=src, scalar1=wsc[:, col:col + 1], scalar2=None, op0=MULT)
 
         def w_quant(u):
             wq[u] = stage.tile([P, 512], U32, name="wq", align_bytes=64)
@@ -168,27 +161,38 @@ def tile_patch_embed_qkv_d4_kernel(tc, x_bytes, x_scale, w_bytes, w_scale, gain,
 
         e = {}
 
-        def product_1(u):
+        def product_1(u, first, last):
             half, g = divmod(u, PASSES)
-            for t in range(4):
-                if g == 0:
-                    e[half, t] = bank(4 * half + t)
-                cols = slice(128 * t, 128 * t + 128)
-                nc.tensor.matmul_mx(
-                    out=e[half, t][:],
-                    lhsT=wq[u][:, cols].bitcast(FP8X4), lhsT_scale=wqs[u][:, cols],
-                    rhs=xq[g][:].bitcast(FP8X4), rhs_scale=xqs[g][:], start=(g == 0), stop=(g == PASSES - 1))
+            for a in range(1 + half):
+                for t in range(4):
+                    cols = slice(128 * t, 128 * t + 128)
+                    if half == 0:
+                        if first:
+                            e[0, t] = bank(t)
+                        toks, dst, start, stop = slice(0, TOK), e[0, t][:], first, last
+                    else:
+                        if first and t % 2 == 0:
+                            e[1, t // 2, a] = bank(4 + 2 * a + t // 2)
+                        toks, dst = slice(IMAGE * a, IMAGE * a + IMAGE), e[1, t // 2, a][:, IMAGE * (t % 2):IMAGE * (t % 2) + IMAGE]
+                        start, stop = first and t % 2 == 0, last and t % 2 == 1
+                    nc.tensor.matmul_mx(
+                        out=dst, lhsT=wq[u][:, cols].bitcast(FP8X4), lhsT_scale=wqs[u][:, cols],
+                        rhs=xq[g][:, toks].bitcast(FP8X4), rhs_scale=xqs[g][:, toks], start=start, stop=stop)
 
         pos_t = keep.tile([P, 2048], BF16, name="pos_t")
 
+        pos_bank = {}
+
         def pos_turn(half):
-            pb = bank(6 + half, BF16)
+            pb = pos_bank[half] = bank(half, BF16)
             for t in range(4):
                 for i in range(2):
                     first = D * i + 512 * half + t
                     at = IMAGE * t + 128 * i
                     nc.tensor.transpose(pb[:, at:at + 128], pos_sb[:, first:first + 509:4], ident_b[:])
-            nc.scalar.copy(out=pos_t[:, 1024 * half:1024 * half + 1024], in_=pb[:])
+
+        def pos_out(half):
+            nc.scalar.copy(out=pos_t[:, 1024 * half:1024 * half + 1024], in_=pos_bank[half][:])
 
         hs = [keep.tile([P, 4 * TOK], BF16, name="hs%d" % h) for h in range(2)]
         hint = [keep.tile([P, 4 * TOK], BF16, name="hint%d" % h, align_bytes=64) for h in range(2)]
@@ -199,8 +203,12 @@ def tile_patch_embed_qkv_d4_kernel(tc, x_bytes, x_scale, w_bytes, w_scale, gain,
             r = lo % IMAGE
             for t in slices:
                 at = 1024 * half + IMAGE * t + r
+                if half == 0:
+                    src = e[0, t][:, lo:hi]
+                else:
+                    src = e[1, t // 2, lo // IMAGE][:, IMAGE * (t % 2) + r:IMAGE * (t % 2) + r + hi - lo]
                 nc.vector.scalar_tensor_tensor(
-                    out=hs[half][:, TOK * t + lo:TOK * t + hi], in0=e[half, t][:, lo:hi],
+                    out=hs[half][:, TOK * t + lo:TOK * t + hi], in0=src,
                     scalar=gain_f[:, 4 * half + t:4 * half + t + 1], in1=pos_t[:, at:at + hi - lo], op0=MULT, op1=ADD)
 
         def h_weave(half, i, n=1):
@@ -215,11 +223,12 @@ def tile_patch_embed_qkv_d4_kernel(tc, x_bytes, x_scale, w_bytes, w_scale, gain,
 
         ob, ot = {}, {}
 
-        def product_2(n):
+        def product_2(n, halves=range(2)):
             i, c = divmod(n, COLUMN_BLOCKS)
-            ob[n] = bank(n % 8)
+            if n not in ob:
+                ob[n] = bank(n % 8)
             toks = slice(128 * i, 128 * i + 128)
-            for h in range(2):
+            for h in halves:
                 nc.tensor.matmul_mx(
                     out=ob[n][:],
                     lhsT=hq[h][:, toks].bitcast(FP8X4), lhsT_scale=hqs[h][:, toks],
@@ -233,58 +242,88 @@ def tile_patch_embed_qkv_d4_kernel(tc, x_bytes, x_scale, w_bytes, w_scale, gain,
                 if sum(STORES[i][:k]) <= c:
                     first, width = sum(STORES[i][:k]), STORES[i][k]
             if c == first:
-                ot[i, first] = outs.tile([P, 1024], F32, name="ot")
+                ot[i, first] = outs.tile([P, 512 * max(map(max, STORES))], F32, name="ot")
             o = ot[i, first]
             at = 512 * (c - first)
             nc.vector.tensor_tensor(out=o[:, at:at + 512], in0=ob[n][:], in1=bias_sb[:, 512 * c:512 * c + 512], op=ADD)
             if c == first + width - 1:
-                nc.sync.dma_start(out=out[128 * i:128 * i + 128, 512 * first:512 * (c + 1)], in_=o[:, 0:512 * width])
+                rows = out.rearrange("(a p i) n -> a i p n", a=2, i=2)[i // 2, i % 2]
+                nc.sync.dma_start(out=rows[:, 512 * first:512 * (c + 1)], in_=o[:, 0:512 * width])
 
         nc.scalar.activation(out=ident_b[:], in_=ident[:], func=COPY)
-        to_widen = list(range(UNITS))
-        for g in range(2):
-            x_widen(g)
-            x_turn(g)
-            w_widen(to_widen.pop(0))
-            if g == 0:
-                pick_w_scales()
-            x_out(g)
-        w_scale_in(0)
-        for s in range(UNITS):
+        for a in range(2):
+            for g in range(2):
+                x_widen(g, a)
+                x_turn(g, a)
+            w_widen(0, slice(2048 * a, 2048 * a + 2048))
+        pick_w_scales()
+        x_out(0, 0)
+        x_widen(2, 0)
+        x_turn(2, 0)
+        w_widen(1)
+        x_out(0, 1)
+        blocks = [(u, b) for u in range(PASSES, UNITS) for b in range(4)]
+        scalar_blocks, vector_blocks = blocks[:SCALAR_BLOCKS], blocks[SCALAR_BLOCKS:]
+        for b in range(4):
+            w_weave(0, b, False)
+        for s in range(PASSES):
             if s + 2 < PASSES:
-                x_widen(s + 2)
-                x_turn(s + 2)
-            for j in range(WIDEN_IN_STEP[s]):
-                w_widen(to_widen.pop(0))
-            if s + 2 < PASSES:
-                x_out(s + 2)
-            if s == 4:
-                nc.scalar.copy(out=gain_f[:], in_=gain_b[:])
+                for a in range(1 if s == 0 else 0, 2):
+                    x_widen(s + 2, a)
+                    x_turn(s + 2, a)
+                w_widen(s + 2)
+            if s == 0:
                 pos_turn(0)
                 pos_turn(1)
-            if s == UNITS - 2:
-                w_quant(s)
-            if s + 1 < UNITS:
-                w_scale_in(s + 1)
-            if s < PASSES:
-                x_quant(s)
-            if s == UNITS - 1:
+            if s + 1 < PASSES:
+                x_out(s + 1, 0)
+                x_out(s + 1, 1)
+            if s == 0:
+                pos_out(0)
+                pos_out(1)
+            for j in range(BLOCKS_IN_STEP[s]):
+                w_weave(*scalar_blocks.pop(0), True)
+            if s + 1 < PASSES:
+                for b in range(4):
+                    w_weave(s + 1, b, False)
+            x_quant(s)
+            w_quant(s)
+            product_1(s, s == 0, s == PASSES - 1)
+
+        nc.scalar.copy(out=gain_f[:], in_=gain_b[:])
+        shared = scalar_blocks[-1][0]
+        scalar_units = list(range(PASSES, shared))
+        vector_units = list(range(UNITS - 1, shared, -1))
+        todo = []
+        for j in range(max(len(scalar_units), len(vector_units))):
+            todo.extend(scalar_units[j:j + 1])
+            todo.extend(vector_units[j:j + 1])
+        todo.append(shared)
+        for j, u in enumerate(todo):
+            for block in [x for x in scalar_blocks if x[0] == u]:
+                w_weave(*block, True)
+            if j + 1 < len(todo):
+                for block in [x for x in vector_blocks if x[0] == todo[j + 1]]:
+                    w_weave(*block, False)
+            if j + 2 == len(todo):
                 h_add(0, 0, IMAGE)
+            if j + 1 == len(todo):
                 h_weave(0, 0, 2)
-            if s != UNITS - 2:
-                w_quant(s)
-            product_1(s)
+            w_quant(u)
+            product_1(u, j == 0, u == shared)
 
         h_add(0, IMAGE, TOK)
         h_add(1, 0, 128)
         h_weave(1, 0)
+        h_quant(0, 0, 2)
+        for n in range(4):
+            product_2(n, range(0, 1))
         h_add(1, 128, IMAGE)
         h_weave(1, 1)
-        h_quant(0, 0, 2)
         h_quant(1, 0)
         h_add(1, IMAGE, TOK, range(0, 2))
         for n in range(4):
-            product_2(n)
+            product_2(n, range(1, 2))
         for n in range(TOKEN_TILES * COLUMN_BLOCKS):
             finish(n)
             if n == 0:

@@ -146,8 +146,9 @@ def tile_patch_embed_qkv_d4_kernel(tc, x_bytes, x_scale, w_bytes, w_scale, gain,
             half, g = divmod(u, PASSES)
             if u not in wint:
                 wint[u] = stage.tile([P, 2048], BF16, name="wint_s" if on_scalar else "wint_v", align_bytes=64)
-            src = ww[g][:].rearrange("p (j b m t) -> p b m j t", j=4, b=8, t=4)[:, 4 * half + b]
-            dst = wint[u][:].rearrange("p (t b m j) -> p b m j t", t=4, b=4, j=4)[:, b]
+            walk = "p b m t j" if on_scalar else "p b m j t"
+            src = ww[g][:].rearrange("p (j b m t) -> " + walk, j=4, b=8, t=4)[:, 4 * half + b]
+            dst = wint[u][:].rearrange("p (t b m j) -> " + walk, t=4, b=4, j=4)[:, b]
             col = 8 * g + 4 * half + b
             if on_scalar:
                 nc.scalar.activation(out=dst, in_=src, func=COPY, scale=wsc[:, col:col + 1])
@@ -213,8 +214,8 @@ def tile_patch_embed_qkv_d4_kernel(tc, x_bytes, x_scale, w_bytes, w_scale, gain,
 
         def h_weave(half, i, n=1):
             nc.scalar.copy(
-                out=hint[half][:, 512 * i:512 * (i + n)].rearrange("p (c r t) -> p c t r", r=4, t=4),
-                in_=hs[half][:].rearrange("p (t c r) -> p c t r", t=4, r=4)[:, 32 * i:32 * (i + n)])
+                out=hint[half][:, 512 * i:512 * (i + n)].rearrange("p (r t) -> p r t", t=4),
+                in_=hs[half][:].rearrange("p (t r) -> p r t", t=4)[:, 128 * i:128 * (i + n)])
 
         def h_quant(half, i, n=1):
             toks = slice(128 * i, 128 * (i + n))

@@ -25,10 +25,10 @@ TOKEN_TILES = TOK // P
 COLUMN_BLOCKS = N // 512
 FLOPS = 2 * TOK * K * D + 2 * TOK * D * N
 
-SCALAR_BLOCKS = 14
-BLOCKS_IN_STEP = (0, 0, 0, 0, 3, 3)
+SCALAR_BLOCKS = 10
+WIDEN_ORDER = (0, 1, 2, 3, 4, 6, 5, 11, 10, 9, 8, 7)
 OUT_BUFS = 5
-STORES = ((1, 1, 2, 2), (2, 2, 2), (2, 2, 2), (2, 2, 1, 1))
+STORES = ((512, 512, 1024, 1024), (1024, 1024, 1024), (1024, 1024, 1024), (1024, 1024, 512, 512))
 
 
 def tile_patch_embed_qkv_d4_kernel(tc, x_bytes, x_scale, w_bytes, w_scale, gain, pos, v_words, v_scales, bias, out):
@@ -51,31 +51,37 @@ def tile_patch_embed_qkv_d4_kernel(tc, x_bytes, x_scale, w_bytes, w_scale, gain,
         nc.scalar.dma_start(out=xs[:].rearrange("p (a c) -> p a c", a=2), in_=x_scale.rearrange("(a p i) c -> p a (i c)", a=2, i=2))
 
         xb = {(a, j): keep.tile([P, 2048], U8, name="xb%d%d" % (a, j)) for a in range(2) for j in range(PASSES // 2)}
-        wb = [keep.tile([P, 4096], U8, name="wb%d" % g) for g in range(PASSES)]
+        wb = [keep.tile([P, 2048], U8, name="wb%d" % u) for u in range(UNITS)]
 
-        def load_x(a, j):
+        def load_x(a, j, tiles=slice(0, 2)):
             nc.sync.dma_start(
-                out=xb[a, j][:].rearrange("p (i k) -> p i k", i=2),
-                in_=x_bytes.rearrange("(a p i) k -> a p i k", a=2, i=2)[a, :, :, 1024 * j:1024 * j + 1024])
+                out=xb[a, j][:].rearrange("p (i k) -> p i k", i=2)[:, tiles],
+                in_=x_bytes.rearrange("(a p i) k -> a p i k", a=2, i=2)[a, :, tiles, 1024 * j:1024 * j + 1024])
 
-        def load_w(g, cols=slice(0, 4096)):
-            nc.sync.dma_start(out=wb[g][:, cols], in_=w_bytes[PASS * g:PASS * g + PASS, :].rearrange("(p t) n -> p (t n)", t=4)[:, cols])
+        def load_w(u):
+            half, g = divmod(u, PASSES)
+            nc.sync.dma_start(
+                out=wb[u][:].rearrange("p (t n) -> p t n", t=4),
+                in_=w_bytes[PASS * g:PASS * g + PASS, 512 * half:512 * half + 512].rearrange("(p t) n -> p t n", t=4))
 
-        load_x(0, 0)
-        load_w(0, slice(0, 2048))
-        load_x(1, 0)
-        load_w(0, slice(2048, 4096))
+        load_x(0, 0, slice(0, 1))
+        load_x(0, 0, slice(1, 2))
+        load_w(0)
+        load_x(1, 0, slice(0, 1))
+        load_x(1, 0, slice(1, 2))
         w_scale_all = keep.tile([P, 192], F32, name="w_scale_all")
         nc.sync.dma_start(out=w_scale_all[:], in_=w_scale.rearrange("c d -> (c d)").partition_broadcast(P))
+        load_w(1)
+        load_x(0, 1)
+        load_w(2)
+        load_x(1, 1)
         pos_sb = keep.tile([P, 2 * D], BF16, name="pos_sb")
-        for g in range(1, PASSES):
-            if g % 2 == 1 and g + 1 < PASSES:
-                load_x(0, (g + 1) // 2)
-            load_w(g)
-            if g % 2 == 1 and g + 1 < PASSES:
-                load_x(1, (g + 1) // 2)
-            if g == 1:
-                nc.sync.dma_start(out=pos_sb[:], in_=pos.rearrange("(p i) j -> p (i j)", i=2))
+        nc.sync.dma_start(out=pos_sb[:], in_=pos.rearrange("(p i) j -> p (i j)", i=2))
+        load_w(3)
+        load_x(0, 2)
+        load_x(1, 2)
+        for u in WIDEN_ORDER[4:]:
+            load_w(u)
         gain_b = keep.tile([P, 8], BF16, name="gain_b")
         nc.sync.dma_start(out=gain_b[:].rearrange("p (h t) -> p h t", h=2), in_=gain.rearrange("(h p t) -> p h t", h=2, t=4))
         vw = [keep.tile([P, 2 * N], U8, name="vw%d" % h, align_bytes=64) for h in range(2)]
@@ -102,10 +108,10 @@ def tile_patch_embed_qkv_d4_kernel(tc, x_bytes, x_scale, w_bytes, w_scale, gain,
 
         xw, xint, xq, xqs, xbank = {}, {}, {}, {}, {}
 
-        def x_widen(g, a):
-            if a == 0:
+        def x_widen(g, a, tiles=range(2)):
+            if g not in xw:
                 xw[g] = stage.tile([P, 2048], BF16, name="xw")
-            for i in range(2):
+            for i in tiles:
                 for c in range(4):
                     at = 1024 * a + 512 * i + 128 * c
                     src = 1024 * i + 512 * (g % 2) + 128 * c
@@ -137,17 +143,16 @@ def tile_patch_embed_qkv_d4_kernel(tc, x_bytes, x_scale, w_bytes, w_scale, gain,
 
         ww, wint, wq, wqs = {}, {}, {}, {}
 
-        def w_widen(g, cols=slice(0, 4096)):
-            if cols.start == 0:
-                ww[g] = keep.tile([P, 4096], BF16, name="ww%d" % g)
-            nc.scalar.copy(out=ww[g][:, cols], in_=wb[g][:, cols].bitcast(FP8))
+        def w_widen(u):
+            ww[u] = keep.tile([P, 2048], BF16, name="ww%d" % u)
+            nc.scalar.copy(out=ww[u][:], in_=wb[u][:].bitcast(FP8))
 
         def w_weave(u, b, on_scalar):
             half, g = divmod(u, PASSES)
             if u not in wint:
                 wint[u] = stage.tile([P, 2048], BF16, name="wint_s" if on_scalar else "wint_v", align_bytes=64)
             walk = "p b m t j" if on_scalar else "p b m j t"
-            src = ww[g][:].rearrange("p (j b m t) -> " + walk, j=4, b=8, t=4)[:, 4 * half + b]
+            src = ww[u][:].rearrange("p (j b m t) -> " + walk, j=4, b=4, t=4)[:, b]
             dst = wint[u][:].rearrange("p (t b m j) -> " + walk, t=4, b=4, j=4)[:, b]
             col = 8 * g + 4 * half + b
             if on_scalar:
@@ -155,10 +160,13 @@ def tile_patch_embed_qkv_d4_kernel(tc, x_bytes, x_scale, w_bytes, w_scale, gain,
             else:
                 nc.vector.tensor_scalar(out=dst, in0=src, scalar1=wsc[:, col:col + 1], scalar2=None, op0=MULT)
 
-        def w_quant(u):
+        def w_quant(u, parts=1):
             wq[u] = stage.tile([P, 512], U32, name="wq", align_bytes=64)
             wqs[u] = stage.tile([P, 512], U8, name="wqs", align_bytes=64)
-            nc.vector.quantize_mx(out=wq[u][:].bitcast(FP8X4), scales=wqs[u][:], in_=wint[u][:])
+            n = 512 // parts
+            for j in range(parts):
+                nc.vector.quantize_mx(
+                    out=wq[u][:, n * j:n * j + n].bitcast(FP8X4), scales=wqs[u][:, n * j:n * j + n], in_=wint[u][:, 4 * n * j:4 * n * (j + 1)])
 
         e = {}
 
@@ -212,8 +220,8 @@ def tile_patch_embed_qkv_d4_kernel(tc, x_bytes, x_scale, w_bytes, w_scale, gain,
                     out=hs[half][:, TOK * t + lo:TOK * t + hi], in0=src,
                     scalar=gain_f[:, 4 * half + t:4 * half + t + 1], in1=pos_t[:, at:at + hi - lo], op0=MULT, op1=ADD)
 
-        def h_weave(half, i, n=1):
-            nc.scalar.copy(
+        def h_weave(half, i, n=1, copy=nc.scalar.copy):
+            copy(
                 out=hint[half][:, 512 * i:512 * (i + n)].rearrange("p (r t) -> p r t", t=4),
                 in_=hs[half][:].rearrange("p (t r) -> p r t", t=4)[:, 128 * i:128 * (i + n)])
 
@@ -238,90 +246,105 @@ def tile_patch_embed_qkv_d4_kernel(tc, x_bytes, x_scale, w_bytes, w_scale, gain,
 
         def finish(n):
             i, c = divmod(n, COLUMN_BLOCKS)
-            first, width = 0, STORES[i][0]
-            for k in range(1, len(STORES[i])):
-                if sum(STORES[i][:k]) <= c:
-                    first, width = sum(STORES[i][:k]), STORES[i][k]
-            if c == first:
-                ot[i, first] = outs.tile([P, 512 * max(map(max, STORES))], F32, name="ot")
-            o = ot[i, first]
-            at = 512 * (c - first)
-            nc.vector.tensor_tensor(out=o[:, at:at + 512], in0=ob[n][:], in1=bias_sb[:, 512 * c:512 * c + 512], op=ADD)
-            if c == first + width - 1:
-                rows = out.rearrange("(a p i) n -> a i p n", a=2, i=2)[i // 2, i % 2]
-                nc.sync.dma_start(out=rows[:, 512 * first:512 * (c + 1)], in_=o[:, 0:512 * width])
+            rows = out.rearrange("(a p i) n -> a i p n", a=2, i=2)[i // 2, i % 2]
+            first = 0
+            for width in STORES[i]:
+                lo, hi = max(first, 512 * c), min(first + width, 512 * c + 512)
+                if lo < hi:
+                    if lo == first:
+                        ot[i, first] = outs.tile([P, max(map(max, STORES))], F32, name="ot")
+                    o = ot[i, first]
+                    nc.vector.tensor_tensor(out=o[:, lo - first:hi - first], in0=ob[n][:, lo - 512 * c:hi - 512 * c], in1=bias_sb[:, lo:hi], op=ADD)
+                    if hi == first + width:
+                        nc.sync.dma_start(out=rows[:, first:hi], in_=o[:, 0:width])
+                first = first + width
 
         nc.scalar.activation(out=ident_b[:], in_=ident[:], func=COPY)
-        for a in range(2):
+        to_widen = list(WIDEN_ORDER)
+        for i in range(2):
             for g in range(2):
-                x_widen(g, a)
-                x_turn(g, a)
-            w_widen(0, slice(2048 * a, 2048 * a + 2048))
+                x_widen(g, 0, range(i, i + 1))
+        x_turn(0, 0)
+        x_turn(1, 0)
+        w_widen(to_widen.pop(0))
+        for i in range(2):
+            for g in range(2):
+                x_widen(g, 1, range(i, i + 1))
+        x_turn(0, 1)
+        x_turn(1, 1)
         pick_w_scales()
+        w_widen(to_widen.pop(0))
         x_out(0, 0)
-        x_widen(2, 0)
-        x_turn(2, 0)
-        w_widen(1)
         x_out(0, 1)
         blocks = [(u, b) for u in range(PASSES, UNITS) for b in range(4)]
         scalar_blocks, vector_blocks = blocks[:SCALAR_BLOCKS], blocks[SCALAR_BLOCKS:]
-        for b in range(4):
-            w_weave(0, b, False)
+        shared = scalar_blocks[-1][0]
+        scalar_units = list(range(PASSES, shared))
+        vector_units = list(range(PASSES)) + list(range(UNITS - 1, shared - 1, -1))
+
+        def vector_weave(u):
+            for b in range(4):
+                if u < PASSES or (u, b) in vector_blocks:
+                    w_weave(u, b, False)
+
+        def scalar_weave(n):
+            for j in range(min(n, len(scalar_blocks))):
+                w_weave(*scalar_blocks.pop(0), True)
+
+        vector_weave(0)
         for s in range(PASSES):
             if s + 2 < PASSES:
-                for a in range(1 if s == 0 else 0, 2):
+                for a in range(2):
                     x_widen(s + 2, a)
                     x_turn(s + 2, a)
-                w_widen(s + 2)
             if s == 0:
                 pos_turn(0)
                 pos_turn(1)
             if s + 1 < PASSES:
                 x_out(s + 1, 0)
                 x_out(s + 1, 1)
+                if s == 3:
+                    scalar_weave(4)
+                else:
+                    w_widen(to_widen.pop(0))
+                    w_widen(to_widen.pop(0))
             if s == 0:
                 pos_out(0)
                 pos_out(1)
-            for j in range(BLOCKS_IN_STEP[s]):
-                w_weave(*scalar_blocks.pop(0), True)
-            if s + 1 < PASSES:
-                for b in range(4):
-                    w_weave(s + 1, b, False)
+            vector_weave(vector_units[s + 1])
             x_quant(s)
             w_quant(s)
             product_1(s, s == 0, s == PASSES - 1)
-
+            if s == PASSES - 2:
+                w_quant(PASSES)
+                product_1(PASSES, True, False)
         nc.scalar.copy(out=gain_f[:], in_=gain_b[:])
-        shared = scalar_blocks[-1][0]
-        scalar_units = list(range(PASSES, shared))
-        vector_units = list(range(UNITS - 1, shared, -1))
-        todo = []
-        for j in range(max(len(scalar_units), len(vector_units))):
-            todo.extend(scalar_units[j:j + 1])
-            todo.extend(vector_units[j:j + 1])
-        todo.append(shared)
-        for j, u in enumerate(todo):
-            for block in [x for x in scalar_blocks if x[0] == u]:
-                w_weave(*block, True)
-            if j + 1 < len(todo):
-                for block in [x for x in vector_blocks if x[0] == todo[j + 1]]:
-                    w_weave(*block, False)
-            if j + 2 == len(todo):
-                h_add(0, 0, IMAGE)
-            if j + 1 == len(todo):
-                h_weave(0, 0, 2)
+        while to_widen:
+            w_widen(to_widen.pop(0))
+        scalar_weave(len(scalar_blocks))
+
+        for j in range(PASSES, len(vector_units) - 1):
+            vector_weave(vector_units[j + 1])
+            w_quant(vector_units[j])
+            product_1(vector_units[j], False, False)
+        for u in scalar_units[1:]:
             w_quant(u)
-            product_1(u, j == 0, u == shared)
+            product_1(u, False, False)
+        h_add(0, 0, IMAGE)
+        h_weave(0, 0, 2)
+        w_quant(shared, 2)
+        product_1(shared, False, True)
 
         h_add(0, IMAGE, TOK)
         h_add(1, 0, 128)
-        h_weave(1, 0)
         h_quant(0, 0, 2)
+        h_weave(1, 0, copy=nc.vector.tensor_copy)
         for n in range(4):
             product_2(n, range(0, 1))
-        h_add(1, 128, IMAGE)
-        h_weave(1, 1)
+        h_add(1, 128, IMAGE, range(0, 2))
         h_quant(1, 0)
+        h_add(1, 128, IMAGE, range(2, 4))
+        h_weave(1, 1)
         h_add(1, IMAGE, TOK, range(0, 2))
         for n in range(4):
             product_2(n, range(1, 2))

@@ -27,7 +27,6 @@ FLOPS = 2 * TOK * K * D + 2 * TOK * D * N
 
 SCALAR_BLOCKS = 10
 WIDEN_ORDER = (0, 1, 2, 3, 4, 6, 5, 11, 10, 9, 8, 7)
-OUT_BUFS = 5
 STORES = ((512, 512, 1024, 1024), (1024, 1024, 1024), (1024, 1024, 1024), (1024, 1024, 512, 512))
 
 
@@ -36,7 +35,7 @@ def tile_patch_embed_qkv_d4_kernel(tc, x_bytes, x_scale, w_bytes, w_scale, gain,
     with ExitStack() as ctx:
         keep = ctx.enter_context(tc.tile_pool(name="keep", bufs=1))
         stage = ctx.enter_context(tc.tile_pool(name="stage", bufs=3))
-        outs = ctx.enter_context(tc.tile_pool(name="outs", bufs=OUT_BUFS))
+        wide = ctx.enter_context(tc.tile_pool(name="wide", bufs=UNITS))
         psum = ctx.enter_context(tc.psum_pool(name="psum", bufs=1))
         ctx.enter_context(tc.manual_schedule())
 
@@ -144,7 +143,7 @@ def tile_patch_embed_qkv_d4_kernel(tc, x_bytes, x_scale, w_bytes, w_scale, gain,
         ww, wint, wq, wqs = {}, {}, {}, {}
 
         def w_widen(u):
-            ww[u] = keep.tile([P, 2048], BF16, name="ww%d" % u)
+            ww[u] = wide.tile([P, 2048], BF16, name="wide")
             nc.scalar.copy(out=ww[u][:], in_=wb[u][:].bitcast(FP8))
 
         def w_weave(u, b, on_scalar):
@@ -252,11 +251,12 @@ def tile_patch_embed_qkv_d4_kernel(tc, x_bytes, x_scale, w_bytes, w_scale, gain,
                 lo, hi = max(first, 512 * c), min(first + width, 512 * c + 512)
                 if lo < hi:
                     if lo == first:
-                        ot[i, first] = outs.tile([P, max(map(max, STORES))], F32, name="ot")
+                        ot[i, first] = wide.tile([P, 1024], F32, name="wide")
                     o = ot[i, first]
                     nc.vector.tensor_tensor(out=o[:, lo - first:hi - first], in0=ob[n][:, lo - 512 * c:hi - 512 * c], in1=bias_sb[:, lo:hi], op=ADD)
                     if hi == first + width:
-                        nc.sync.dma_start(out=rows[:, first:hi], in_=o[:, 0:width])
+                        queue = nc.scalar if i > 0 and first // 1024 % 2 == i % 2 else nc.sync
+                        queue.dma_start(out=rows[:, first:hi], in_=o[:, 0:width])
                 first = first + width
 
         nc.scalar.activation(out=ident_b[:], in_=ident[:], func=COPY)

@@ -26,7 +26,8 @@ COLUMN_BLOCKS = N // 512
 FLOPS = 2 * TOK * K * D + 2 * TOK * D * N
 
 SCALAR_BLOCKS = 10
-WIDEN_ORDER = (0, 1, 2, 3, 4, 6, 5, 11, 10, 9, 8, 7)
+SPLIT_PASSES = 2
+HALF_1 = (8, 6, 7, 9, 10, 11)
 STORES = ((512, 512, 1024, 1024), (1024, 1024, 1024), (1024, 1024, 1024), (1024, 1024, 512, 512))
 
 
@@ -35,7 +36,7 @@ def tile_patch_embed_qkv_d4_kernel(tc, x_bytes, x_scale, w_bytes, w_scale, gain,
     with ExitStack() as ctx:
         keep = ctx.enter_context(tc.tile_pool(name="keep", bufs=1))
         stage = ctx.enter_context(tc.tile_pool(name="stage", bufs=3))
-        wide = ctx.enter_context(tc.tile_pool(name="wide", bufs=UNITS))
+        wide = ctx.enter_context(tc.tile_pool(name="wide", bufs=4))
         psum = ctx.enter_context(tc.psum_pool(name="psum", bufs=1))
         ctx.enter_context(tc.manual_schedule())
 
@@ -50,7 +51,7 @@ def tile_patch_embed_qkv_d4_kernel(tc, x_bytes, x_scale, w_bytes, w_scale, gain,
         nc.scalar.dma_start(out=xs[:].rearrange("p (a c) -> p a c", a=2), in_=x_scale.rearrange("(a p i) c -> p a (i c)", a=2, i=2))
 
         xb = {(a, j): keep.tile([P, 2048], U8, name="xb%d%d" % (a, j)) for a in range(2) for j in range(PASSES // 2)}
-        wb = [keep.tile([P, 2048], U8, name="wb%d" % u) for u in range(UNITS)]
+        wb = {}
 
         def load_x(a, j, tiles=slice(0, 2)):
             nc.sync.dma_start(
@@ -59,9 +60,15 @@ def tile_patch_embed_qkv_d4_kernel(tc, x_bytes, x_scale, w_bytes, w_scale, gain,
 
         def load_w(u):
             half, g = divmod(u, PASSES)
-            nc.sync.dma_start(
-                out=wb[u][:].rearrange("p (t n) -> p t n", t=4),
-                in_=w_bytes[PASS * g:PASS * g + PASS, 512 * half:512 * half + 512].rearrange("(p t) n -> p t n", t=4))
+            rows = w_bytes[PASS * g:PASS * g + PASS, :]
+            if g < SPLIT_PASSES:
+                wb[u] = keep.tile([P, 2048], U8, name="wb%d" % u)
+                nc.sync.dma_start(
+                    out=wb[u][:].rearrange("p (t n) -> p t n", t=4),
+                    in_=rows[:, 512 * half:512 * half + 512].rearrange("(p t) n -> p t n", t=4))
+            else:
+                wb[u] = keep.tile([P, 4096], U8, name="wb%d" % u)
+                nc.sync.dma_start(out=wb[u][:], in_=rows.rearrange("(p t) n -> p (t n)", t=4))
 
         load_x(0, 0, slice(0, 1))
         load_x(0, 0, slice(1, 2))
@@ -72,14 +79,14 @@ def tile_patch_embed_qkv_d4_kernel(tc, x_bytes, x_scale, w_bytes, w_scale, gain,
         nc.sync.dma_start(out=w_scale_all[:], in_=w_scale.rearrange("c d -> (c d)").partition_broadcast(P))
         load_w(1)
         load_x(0, 1)
-        load_w(2)
         load_x(1, 1)
+        load_w(2)
         pos_sb = keep.tile([P, 2 * D], BF16, name="pos_sb")
         nc.sync.dma_start(out=pos_sb[:], in_=pos.rearrange("(p i) j -> p (i j)", i=2))
         load_w(3)
         load_x(0, 2)
         load_x(1, 2)
-        for u in WIDEN_ORDER[4:]:
+        for u in (4, 5, 6, 7):
             load_w(u)
         gain_b = keep.tile([P, 8], BF16, name="gain_b")
         nc.sync.dma_start(out=gain_b[:].rearrange("p (h t) -> p h t", h=2), in_=gain.rearrange("(h p t) -> p h t", h=2, t=4))
@@ -87,7 +94,7 @@ def tile_patch_embed_qkv_d4_kernel(tc, x_bytes, x_scale, w_bytes, w_scale, gain,
         for h in range(2):
             nc.sync.dma_start(out=vw[h][:].bitcast(I32), in_=v_words[h].bitcast(I32))
         vs = keep.tile([P, 2 * N], U8, name="vs", align_bytes=64)
-        nc.gpsimd.memset(vs[:].bitcast(I32), 0)
+        nc.vector.memset(vs[:].bitcast(I32), 0)
         for q in range(4):
             nc.sync.dma_start(
                 out=vs[32 * q:32 * q + 4, :].rearrange("p (h n) -> p h n", h=2).bitcast(I32),
@@ -143,15 +150,21 @@ def tile_patch_embed_qkv_d4_kernel(tc, x_bytes, x_scale, w_bytes, w_scale, gain,
         ww, wint, wq, wqs = {}, {}, {}, {}
 
         def w_widen(u):
-            ww[u] = wide.tile([P, 2048], BF16, name="wide")
-            nc.scalar.copy(out=ww[u][:], in_=wb[u][:].bitcast(FP8))
+            if u % PASSES < SPLIT_PASSES:
+                tile = wide.tile([P, 2048], BF16, name="wide_unit")
+                ww[u] = tile[:].rearrange("p (t n) -> p t n", t=4)
+            else:
+                tile = wide.tile([P, 4096], BF16, name="wide_pass")
+                both = tile[:].rearrange("p (t n) -> p t n", t=4)
+                ww[u], ww[u + PASSES] = both[:, :, 0:512], both[:, :, 512:1024]
+            nc.scalar.copy(out=tile[:], in_=wb[u][:].bitcast(FP8))
 
         def w_weave(u, b, on_scalar):
             half, g = divmod(u, PASSES)
             if u not in wint:
                 wint[u] = stage.tile([P, 2048], BF16, name="wint_s" if on_scalar else "wint_v", align_bytes=64)
             walk = "p b m t j" if on_scalar else "p b m j t"
-            src = ww[u][:].rearrange("p (j b m t) -> " + walk, j=4, b=4, t=4)[:, b]
+            src = ww[u].rearrange("p j (b m t) -> " + walk, b=4, t=4)[:, b]
             dst = wint[u][:].rearrange("p (t b m j) -> " + walk, t=4, b=4, j=4)[:, b]
             col = 8 * g + 4 * half + b
             if on_scalar:
@@ -251,7 +264,7 @@ def tile_patch_embed_qkv_d4_kernel(tc, x_bytes, x_scale, w_bytes, w_scale, gain,
                 lo, hi = max(first, 512 * c), min(first + width, 512 * c + 512)
                 if lo < hi:
                     if lo == first:
-                        ot[i, first] = wide.tile([P, 1024], F32, name="wide")
+                        ot[i, first] = wide.tile([P, 1024], F32, name="wide_unit" if len(ot) % 2 else "wide_pass")
                     o = ot[i, first]
                     nc.vector.tensor_tensor(out=o[:, lo - first:hi - first], in0=ob[n][:, lo - 512 * c:hi - 512 * c], in1=bias_sb[:, lo:hi], op=ADD)
                     if hi == first + width:
@@ -260,27 +273,26 @@ def tile_patch_embed_qkv_d4_kernel(tc, x_bytes, x_scale, w_bytes, w_scale, gain,
                 first = first + width
 
         nc.scalar.activation(out=ident_b[:], in_=ident[:], func=COPY)
-        to_widen = list(WIDEN_ORDER)
         for i in range(2):
             for g in range(2):
                 x_widen(g, 0, range(i, i + 1))
         x_turn(0, 0)
         x_turn(1, 0)
-        w_widen(to_widen.pop(0))
+        w_widen(0)
         for i in range(2):
             for g in range(2):
                 x_widen(g, 1, range(i, i + 1))
         x_turn(0, 1)
         x_turn(1, 1)
         pick_w_scales()
-        w_widen(to_widen.pop(0))
+        w_widen(1)
         x_out(0, 0)
         x_out(0, 1)
-        blocks = [(u, b) for u in range(PASSES, UNITS) for b in range(4)]
+        blocks = [(u, b) for u in HALF_1 for b in range(4)]
         scalar_blocks, vector_blocks = blocks[:SCALAR_BLOCKS], blocks[SCALAR_BLOCKS:]
         shared = scalar_blocks[-1][0]
-        scalar_units = list(range(PASSES, shared))
-        vector_units = list(range(PASSES)) + list(range(UNITS - 1, shared - 1, -1))
+        scalar_units = list(HALF_1[:list(HALF_1).index(shared)])
+        vector_units = list(range(PASSES)) + list(reversed(HALF_1[list(HALF_1).index(shared):]))
 
         def vector_weave(u):
             for b in range(4):
@@ -300,14 +312,17 @@ def tile_patch_embed_qkv_d4_kernel(tc, x_bytes, x_scale, w_bytes, w_scale, gain,
             if s == 0:
                 pos_turn(0)
                 pos_turn(1)
+            if s + 2 < PASSES:
+                w_widen(s + 2)
             if s + 1 < PASSES:
                 x_out(s + 1, 0)
                 x_out(s + 1, 1)
-                if s == 3:
-                    scalar_weave(4)
-                else:
-                    w_widen(to_widen.pop(0))
-                    w_widen(to_widen.pop(0))
+            if s + 2 == PASSES:
+                scalar_weave(4)
+                w_widen(PASSES)
+                w_widen(PASSES + 1)
+                nc.scalar.copy(out=gain_f[:], in_=gain_b[:])
+                scalar_weave(len(scalar_blocks))
             if s == 0:
                 pos_out(0)
                 pos_out(1)
@@ -315,14 +330,9 @@ def tile_patch_embed_qkv_d4_kernel(tc, x_bytes, x_scale, w_bytes, w_scale, gain,
             x_quant(s)
             w_quant(s)
             product_1(s, s == 0, s == PASSES - 1)
-            if s == PASSES - 2:
-                w_quant(PASSES)
-                product_1(PASSES, True, False)
-        nc.scalar.copy(out=gain_f[:], in_=gain_b[:])
-        while to_widen:
-            w_widen(to_widen.pop(0))
-        scalar_weave(len(scalar_blocks))
 
+        w_quant(scalar_units[0])
+        product_1(scalar_units[0], True, False)
         for j in range(PASSES, len(vector_units) - 1):
             vector_weave(vector_units[j + 1])
             w_quant(vector_units[j])

@@ -25,7 +25,7 @@ TOKEN_TILES = TOK // P
 COLUMN_BLOCKS = N // 512
 FLOPS = 2 * TOK * K * D + 2 * TOK * D * N
 
-SCALAR_BLOCKS = 10
+SCALAR_BLOCKS = 11
 SPLIT_PASSES = 2
 HALF_1 = (8, 6, 7, 9, 10, 11)
 STORES = ((512, 512, 1024, 1024), (1024, 1024, 1024), (1024, 1024, 1024), (1024, 1024, 512, 512))
@@ -45,10 +45,12 @@ def tile_patch_embed_qkv_d4_kernel(tc, x_bytes, x_scale, w_bytes, w_scale, gain,
 
         ident = keep.tile([P, P], F32, name="ident")
         make_identity(nc, ident[:])
-        ident_b = keep.tile([P, P], BF16, name="ident_b")
 
         xs = keep.tile([P, TOKEN_TILES * 24], F32, name="xs")
         nc.scalar.dma_start(out=xs[:].rearrange("p (a c) -> p a c", a=2), in_=x_scale.rearrange("(a p i) c -> p a (i c)", a=2, i=2))
+
+        gain_b = keep.tile([P, 8], BF16, name="gain_b")
+        nc.scalar.dma_start(out=gain_b[:].rearrange("p (h t) -> p h t", h=2), in_=gain.rearrange("(h p t) -> p h t", h=2, t=4))
 
         xb = {(a, j): keep.tile([P, 2048], U8, name="xb%d%d" % (a, j)) for a in range(2) for j in range(PASSES // 2)}
         wb = {}
@@ -81,15 +83,13 @@ def tile_patch_embed_qkv_d4_kernel(tc, x_bytes, x_scale, w_bytes, w_scale, gain,
         load_x(0, 1)
         load_x(1, 1)
         load_w(2)
-        pos_sb = keep.tile([P, 2 * D], BF16, name="pos_sb")
-        nc.sync.dma_start(out=pos_sb[:], in_=pos.rearrange("(p i) j -> p (i j)", i=2))
         load_w(3)
         load_x(0, 2)
         load_x(1, 2)
         for u in (4, 5, 6, 7):
             load_w(u)
-        gain_b = keep.tile([P, 8], BF16, name="gain_b")
-        nc.sync.dma_start(out=gain_b[:].rearrange("p (h t) -> p h t", h=2), in_=gain.rearrange("(h p t) -> p h t", h=2, t=4))
+        pos_sb = keep.tile([P, 2 * D], BF16, name="pos_sb")
+        nc.sync.dma_start(out=pos_sb[:], in_=pos.rearrange("(p i) j -> p (i j)", i=2))
         vw = [keep.tile([P, 2 * N], U8, name="vw%d" % h, align_bytes=64) for h in range(2)]
         for h in range(2):
             nc.sync.dma_start(out=vw[h][:].bitcast(I32), in_=v_words[h].bitcast(I32))
@@ -182,10 +182,10 @@ def tile_patch_embed_qkv_d4_kernel(tc, x_bytes, x_scale, w_bytes, w_scale, gain,
 
         e = {}
 
-        def product_1(u, first, last):
+        def product_1(u, first, last, slices=range(4)):
             half, g = divmod(u, PASSES)
             for a in range(1 + half):
-                for t in range(4):
+                for t in slices:
                     cols = slice(128 * t, 128 * t + 128)
                     if half == 0:
                         if first:
@@ -201,19 +201,19 @@ def tile_patch_embed_qkv_d4_kernel(tc, x_bytes, x_scale, w_bytes, w_scale, gain,
                         rhs=xq[g][:, toks].bitcast(FP8X4), rhs_scale=xqs[g][:, toks], start=start, stop=stop)
 
         pos_t = keep.tile([P, 2048], BF16, name="pos_t")
-
         pos_bank = {}
 
         def pos_turn(half):
-            pb = pos_bank[half] = bank(half, BF16)
-            for t in range(4):
+            pos_bank[half] = bank(4 + half)
+            words = pos_sb[:].bitcast(F32)
+            for u in range(2):
                 for i in range(2):
-                    first = D * i + 512 * half + t
-                    at = IMAGE * t + 128 * i
-                    nc.tensor.transpose(pb[:, at:at + 128], pos_sb[:, first:first + 509:4], ident_b[:])
+                    first = 512 * i + 256 * half + u
+                    at = IMAGE * u + 128 * i
+                    nc.tensor.transpose(pos_bank[half][:, at:at + 128], words[:, first:first + 255:2], ident[:])
 
         def pos_out(half):
-            nc.scalar.copy(out=pos_t[:, 1024 * half:1024 * half + 1024], in_=pos_bank[half][:])
+            nc.scalar.copy(out=pos_t[:, 1024 * half:1024 * half + 1024].bitcast(F32), in_=pos_bank[half][:])
 
         hs = [keep.tile([P, 4 * TOK], BF16, name="hs%d" % h) for h in range(2)]
         hint = [keep.tile([P, 4 * TOK], BF16, name="hint%d" % h, align_bytes=64) for h in range(2)]
@@ -223,14 +223,14 @@ def tile_patch_embed_qkv_d4_kernel(tc, x_bytes, x_scale, w_bytes, w_scale, gain,
         def h_add(half, lo, hi, slices=range(4)):
             r = lo % IMAGE
             for t in slices:
-                at = 1024 * half + IMAGE * t + r
+                at = 1024 * half + 2 * IMAGE * (t // 2) + 2 * r + t % 2
                 if half == 0:
                     src = e[0, t][:, lo:hi]
                 else:
                     src = e[1, t // 2, lo // IMAGE][:, IMAGE * (t % 2) + r:IMAGE * (t % 2) + r + hi - lo]
                 nc.vector.scalar_tensor_tensor(
                     out=hs[half][:, TOK * t + lo:TOK * t + hi], in0=src,
-                    scalar=gain_f[:, 4 * half + t:4 * half + t + 1], in1=pos_t[:, at:at + hi - lo], op0=MULT, op1=ADD)
+                    scalar=gain_f[:, 4 * half + t:4 * half + t + 1], in1=pos_t[:, at:at + 2 * (hi - lo) - 1:2], op0=MULT, op1=ADD)
 
         def h_weave(half, i, n=1, copy=nc.scalar.copy):
             copy(
@@ -272,7 +272,7 @@ def tile_patch_embed_qkv_d4_kernel(tc, x_bytes, x_scale, w_bytes, w_scale, gain,
                         queue.dma_start(out=rows[:, first:hi], in_=o[:, 0:width])
                 first = first + width
 
-        nc.scalar.activation(out=ident_b[:], in_=ident[:], func=COPY)
+        nc.scalar.activation(out=gain_f[:], in_=gain_b[:], func=COPY)
         for i in range(2):
             for g in range(2):
                 x_widen(g, 0, range(i, i + 1))
@@ -309,27 +309,28 @@ def tile_patch_embed_qkv_d4_kernel(tc, x_bytes, x_scale, w_bytes, w_scale, gain,
                 for a in range(2):
                     x_widen(s + 2, a)
                     x_turn(s + 2, a)
-            if s == 0:
-                pos_turn(0)
-                pos_turn(1)
+            if s > 0:
+                product_1(s - 1, s == 1, False, range(2, 4))
             if s + 2 < PASSES:
                 w_widen(s + 2)
             if s + 1 < PASSES:
                 x_out(s + 1, 0)
                 x_out(s + 1, 1)
+            if s + 3 == PASSES:
+                pos_turn(0)
+                pos_turn(1)
+            if s + 2 == PASSES:
+                pos_out(0)
+                pos_out(1)
             if s + 2 == PASSES:
                 scalar_weave(4)
                 w_widen(PASSES)
                 w_widen(PASSES + 1)
-                nc.scalar.copy(out=gain_f[:], in_=gain_b[:])
                 scalar_weave(len(scalar_blocks))
-            if s == 0:
-                pos_out(0)
-                pos_out(1)
             vector_weave(vector_units[s + 1])
             x_quant(s)
             w_quant(s)
-            product_1(s, s == 0, s == PASSES - 1)
+            product_1(s, s == 0, s == PASSES - 1, range(0, 2) if s + 1 < PASSES else range(4))
 
         w_quant(scalar_units[0])
         product_1(scalar_units[0], True, False)
@@ -349,15 +350,16 @@ def tile_patch_embed_qkv_d4_kernel(tc, x_bytes, x_scale, w_bytes, w_scale, gain,
         h_add(1, 0, 128)
         h_quant(0, 0, 2)
         h_weave(1, 0, copy=nc.vector.tensor_copy)
-        for n in range(4):
+        for n in range(3):
             product_2(n, range(0, 1))
         h_add(1, 128, IMAGE, range(0, 2))
         h_quant(1, 0)
         h_add(1, 128, IMAGE, range(2, 4))
         h_weave(1, 1)
         h_add(1, IMAGE, TOK, range(0, 2))
-        for n in range(4):
+        for n in range(3):
             product_2(n, range(1, 2))
+        product_2(3)
         for n in range(TOKEN_TILES * COLUMN_BLOCKS):
             finish(n)
             if n == 0:

@@ -25,7 +25,7 @@ TOKEN_TILES = TOK // P
 COLUMN_BLOCKS = N // 512
 FLOPS = 2 * TOK * K * D + 2 * TOK * D * N
 
-SCALAR_BLOCKS = 11
+SCALAR_BLOCKS = 12
 SPLIT_PASSES = 2
 HALF_1 = (8, 6, 7, 9, 10, 11)
 STORES = ((512, 512, 1024, 1024), (1024, 1024, 1024), (1024, 1024, 1024), (1024, 1024, 512, 512))
@@ -119,11 +119,12 @@ def tile_patch_embed_qkv_d4_kernel(tc, x_bytes, x_scale, w_bytes, w_scale, gain,
                 xw[g] = stage.tile([P, 2048], BF16, name="xw")
             for i in tiles:
                 for c in range(4):
-                    at = 1024 * a + 512 * i + 128 * c
+                    at = 1024 * a + 512 * i
                     src = 1024 * i + 512 * (g % 2) + 128 * c
                     col = 24 * (2 * a + i) + 4 * g + c
                     nc.vector.tensor_scalar(
-                        out=xw[g][:, at:at + 128], in0=xb[a, g // 2][:, src:src + 128].bitcast(FP8),
+                        out=xw[g][:, at:at + 512].rearrange("p (u c q e) -> p c q u e", u=2, c=4, e=2)[:, c],
+                        in0=xb[a, g // 2][:, src:src + 128].bitcast(FP8).rearrange("p (q u e) -> p q u e", u=2, e=2),
                         scalar1=xs[:, col:col + 1], scalar2=None, op0=MULT)
 
         def x_turn(g, a):
@@ -131,9 +132,9 @@ def tile_patch_embed_qkv_d4_kernel(tc, x_bytes, x_scale, w_bytes, w_scale, gain,
             xbank[g, a] = bank(4 + (2 * g + a) % 4)
             for i in range(2):
                 for u in range(2):
-                    first = 256 * (2 * a + i) + u
+                    first = 256 * (2 * a + i) + 128 * u
                     at = 128 * (2 * i + u)
-                    nc.tensor.transpose(xbank[g, a][:, at:at + 128], words[:, first:first + 255:2], ident[:])
+                    nc.tensor.transpose(xbank[g, a][:, at:at + 128], words[:, first:first + 128], ident[:])
 
         def x_out(g, a):
             if a == 0:
@@ -319,12 +320,12 @@ def tile_patch_embed_qkv_d4_kernel(tc, x_bytes, x_scale, w_bytes, w_scale, gain,
             if s + 3 == PASSES:
                 pos_turn(0)
                 pos_turn(1)
+                w_widen(PASSES)
             if s + 2 == PASSES:
+                scalar_weave(2)
                 pos_out(0)
                 pos_out(1)
-            if s + 2 == PASSES:
-                scalar_weave(4)
-                w_widen(PASSES)
+                scalar_weave(2)
                 w_widen(PASSES + 1)
                 scalar_weave(len(scalar_blocks))
             vector_weave(vector_units[s + 1])
@@ -332,21 +333,28 @@ def tile_patch_embed_qkv_d4_kernel(tc, x_bytes, x_scale, w_bytes, w_scale, gain,
             w_quant(s)
             product_1(s, s == 0, s == PASSES - 1, range(0, 2) if s + 1 < PASSES else range(4))
 
-        w_quant(scalar_units[0])
-        product_1(scalar_units[0], True, False)
-        for j in range(PASSES, len(vector_units) - 1):
-            vector_weave(vector_units[j + 1])
-            w_quant(vector_units[j])
-            product_1(vector_units[j], False, False)
-        for u in scalar_units[1:]:
+        def quant_and_multiply(u, first=False):
             w_quant(u)
-            product_1(u, False, False)
-        h_add(0, 0, IMAGE)
+            product_1(u, first, False)
+
+        quant_and_multiply(vector_units[PASSES], True)
+        between = [range(0, 2), range(2, 4)]
+        for u in vector_units[PASSES + 1:]:
+            vector_weave(u)
+            if scalar_units:
+                quant_and_multiply(scalar_units.pop(0))
+            if u != shared:
+                quant_and_multiply(u)
+            if between:
+                h_add(0, 0, IMAGE, between.pop(0))
+        for u in scalar_units:
+            quant_and_multiply(u)
         h_weave(0, 0, 2)
+        h_add(0, IMAGE, TOK, range(0, 1))
         w_quant(shared, 2)
         product_1(shared, False, True)
 
-        h_add(0, IMAGE, TOK)
+        h_add(0, IMAGE, TOK, range(1, 4))
         h_add(1, 0, 128)
         h_quant(0, 0, 2)
         h_weave(1, 0, copy=nc.vector.tensor_copy)

@@ -25,9 +25,17 @@ TOKEN_TILES = TOK // P
 COLUMN_BLOCKS = N // 512
 FLOPS = 2 * TOK * K * D + 2 * TOK * D * N
 
-SCALAR_BLOCKS = 12
+EARLY = 4
+SCALAR_BLOCKS = 13
+LAID = ()
 SPLIT_PASSES = 2
+EXTRA = (1,)
 HALF_1 = (8, 6, 7, 9, 10, 11)
+GPSIMD_TILES = ()
+SCALAR_STORES = (15, 19, 22)
+LATE_STORE = 7
+Q2 = 3
+Q3 = 13
 STORES = ((512, 512, 1024, 1024), (1024, 1024, 1024), (1024, 1024, 1024), (1024, 1024, 512, 512))
 
 
@@ -43,49 +51,72 @@ def tile_patch_embed_qkv_d4_kernel(tc, x_bytes, x_scale, w_bytes, w_scale, gain,
         def bank(b, dtype=F32):
             return psum.tile([P, 512 if dtype == F32 else 1024], dtype, name="bank%d" % b)
 
+        ring = list(range(8))
+
+        def next_bank(dtype=F32):
+            b = ring.pop(0)
+            ring.append(b)
+            return bank(b, dtype)
+
+        held = {}
+
+        def hold_bank(key):
+            held[key] = ring.pop(0)
+            return bank(held[key])
+
+        def free_bank(key):
+            ring.append(held.pop(key))
+
         ident = keep.tile([P, P], F32, name="ident")
         make_identity(nc, ident[:])
+        ident_b = keep.tile([P, P], BF16, name="ident_b")
+        if LAID:
+            make_identity(nc, ident_b[:])
 
         xs = keep.tile([P, TOKEN_TILES * 24], F32, name="xs")
         nc.scalar.dma_start(out=xs[:].rearrange("p (a c) -> p a c", a=2), in_=x_scale.rearrange("(a p i) c -> p a (i c)", a=2, i=2))
-
         gain_b = keep.tile([P, 8], BF16, name="gain_b")
         nc.scalar.dma_start(out=gain_b[:].rearrange("p (h t) -> p h t", h=2), in_=gain.rearrange("(h p t) -> p h t", h=2, t=4))
 
-        xb = {(a, j): keep.tile([P, 2048], U8, name="xb%d%d" % (a, j)) for a in range(2) for j in range(PASSES // 2)}
+        x_rows = x_bytes.rearrange("(a p i) k -> a p i k", a=2, i=2)
+        xb = {}
         wb = {}
 
-        def load_x(a, j, tiles=slice(0, 2)):
-            nc.sync.dma_start(
-                out=xb[a, j][:].rearrange("p (i k) -> p i k", i=2)[:, tiles],
-                in_=x_bytes.rearrange("(a p i) k -> a p i k", a=2, i=2)[a, :, tiles, 1024 * j:1024 * j + 1024])
+        def load_x(tiles, pair):
+            t = keep.tile([P, 1024 * len(tiles)], U8, name="xb%d%d" % (tiles[0], pair))
+            nc.sync.dma_start(out=t[:].rearrange("p (j k) -> p j k", k=1024), in_=x_rows[tiles[0] // 2, :, tiles[0] % 2:tiles[-1] % 2 + 1, 1024 * pair:1024 * pair + 1024])
+            for n, j in enumerate(tiles):
+                xb[j, pair] = t[:, 1024 * n:1024 * n + 1024]
 
-        def load_w(u):
+        def load_w(u, rows_t=slice(0, 4)):
             half, g = divmod(u, PASSES)
             rows = w_bytes[PASS * g:PASS * g + PASS, :]
             if g < SPLIT_PASSES:
-                wb[u] = keep.tile([P, 2048], U8, name="wb%d" % u)
+                if u not in wb:
+                    wb[u] = keep.tile([P, 2048], U8, name="wb%d" % u)
                 nc.sync.dma_start(
-                    out=wb[u][:].rearrange("p (t n) -> p t n", t=4),
-                    in_=rows[:, 512 * half:512 * half + 512].rearrange("(p t) n -> p t n", t=4))
+                    out=wb[u][:].rearrange("p (t n) -> p t n", t=4)[:, rows_t],
+                    in_=rows[:, 512 * half:512 * half + 512].rearrange("(p t) n -> p t n", t=4)[:, rows_t])
             else:
                 wb[u] = keep.tile([P, 4096], U8, name="wb%d" % u)
                 nc.sync.dma_start(out=wb[u][:], in_=rows.rearrange("(p t) n -> p (t n)", t=4))
 
-        load_x(0, 0, slice(0, 1))
-        load_x(0, 0, slice(1, 2))
-        load_w(0)
-        load_x(1, 0, slice(0, 1))
-        load_x(1, 0, slice(1, 2))
-        w_scale_all = keep.tile([P, 192], F32, name="w_scale_all")
-        nc.sync.dma_start(out=w_scale_all[:], in_=w_scale.rearrange("c d -> (c d)").partition_broadcast(P))
+        load_x([0], 0)
+        load_w(0, slice(0, 2))
+        load_x([1], 0)
+        load_w(0, slice(2, 4))
+        load_x([2], 0)
+        load_x([3], 0)
         load_w(1)
-        load_x(0, 1)
-        load_x(1, 1)
+        wsc = keep.tile([P, 168], F32, name="wsc")
+        for q in range(4):
+            nc.sync.dma_start(out=wsc[32 * q:32 * q + 32, :], in_=w_scale.rearrange("c d -> (c d)")[8 * q:8 * q + 168].partition_broadcast(32))
+        load_x([0, 1], 1)
+        load_x([2, 3], 1)
         load_w(2)
         load_w(3)
-        load_x(0, 2)
-        load_x(1, 2)
+        load_x([0, 1], 2)
+        load_x([2, 3], 2)
         for u in (4, 5, 6, 7):
             load_w(u)
         pos_sb = keep.tile([P, 2 * D], BF16, name="pos_sb")
@@ -102,55 +133,47 @@ def tile_patch_embed_qkv_d4_kernel(tc, x_bytes, x_scale, w_bytes, w_scale, gain,
         bias_sb = keep.tile([P, N], BF16, name="bias_sb")
         nc.sync.dma_start(out=bias_sb[:], in_=bias.partition_broadcast(P))
 
-        wsc = keep.tile([P, 8 * PASSES], F32, name="wsc")
         gain_f = keep.tile([P, 8], F32, name="gain_f")
-
-        def pick_w_scales():
-            for q in range(4):
-                rows = slice(32 * q, 32 * q + 32)
-                nc.scalar.copy(
-                    out=wsc[rows, :].rearrange("p (g d) -> p g d", d=8),
-                    in_=w_scale_all[rows, :].rearrange("p (g q d) -> p q g d", q=4, d=8)[:, q])
 
         xw, xint, xq, xqs, xbank = {}, {}, {}, {}, {}
 
-        def x_widen(g, a, tiles=range(2)):
+        def x_widen(g, tiles):
             if g not in xw:
-                xw[g] = stage.tile([P, 2048], BF16, name="xw")
-            for i in tiles:
+                xw[g] = stage.tile([P, 512 * EARLY], BF16, name="xw")
+            for j in tiles:
                 for c in range(4):
-                    at = 1024 * a + 512 * i
-                    src = 1024 * i + 512 * (g % 2) + 128 * c
-                    col = 24 * (2 * a + i) + 4 * g + c
+                    src = 512 * (g % 2) + 128 * c
+                    col = 24 * j + 4 * g + c
                     nc.vector.tensor_scalar(
-                        out=xw[g][:, at:at + 512].rearrange("p (u c q e) -> p c q u e", u=2, c=4, e=2)[:, c],
-                        in0=xb[a, g // 2][:, src:src + 128].bitcast(FP8).rearrange("p (q u e) -> p q u e", u=2, e=2),
+                        out=xw[g][:, 512 * j:512 * j + 512].rearrange("p (u c q e) -> p c q u e", u=2, c=4, e=2)[:, c],
+                        in0=xb[j, g // 2][:, src:src + 128].bitcast(FP8).rearrange("p (q u e) -> p q u e", u=2, e=2),
                         scalar1=xs[:, col:col + 1], scalar2=None, op0=MULT)
 
-        def x_turn(g, a):
+        def x_turn(g, tiles):
             words = xw[g][:].bitcast(F32)
-            xbank[g, a] = bank(4 + (2 * g + a) % 4)
-            for i in range(2):
+            xbank[g, tiles[0]] = next_bank()
+            for n, j in enumerate(tiles):
                 for u in range(2):
-                    first = 256 * (2 * a + i) + 128 * u
-                    at = 128 * (2 * i + u)
-                    nc.tensor.transpose(xbank[g, a][:, at:at + 128], words[:, first:first + 128], ident[:])
+                    first = 256 * j + 128 * u
+                    at = 128 * (2 * n + u)
+                    nc.tensor.transpose(xbank[g, tiles[0]][:, at:at + 128], words[:, first:first + 128], ident[:])
 
-        def x_out(g, a):
-            if a == 0:
-                xint[g] = stage.tile([P, 2048], BF16, name="xint", align_bytes=64)
+        def x_out(g, tiles):
+            if g not in xint:
+                xint[g] = stage.tile([P, 512 * EARLY], BF16, name="xint", align_bytes=64)
+            n = len(tiles)
             nc.scalar.copy(
-                out=xint[g][:, 1024 * a:1024 * a + 1024].bitcast(F32).rearrange("p (i r u) -> p i r u", i=2, u=2),
-                in_=xbank[g, a][:].rearrange("p (i u r) -> p i r u", i=2, u=2))
+                out=xint[g][:, 512 * tiles[0]:512 * (tiles[0] + n)].bitcast(F32).rearrange("p (i r u) -> p i r u", i=n, u=2),
+                in_=xbank[g, tiles[0]][:, 0:256 * n].rearrange("p (i u r) -> p i r u", i=n, u=2))
 
         def x_quant(g):
-            xq[g] = keep.tile([P, TOK], U32, name="xq%d" % g, align_bytes=64)
-            xqs[g] = keep.tile([P, TOK], U8, name="xqs%d" % g, align_bytes=64)
+            xq[g] = keep.tile([P, 128 * EARLY], U32, name="xq%d" % g, align_bytes=64)
+            xqs[g] = keep.tile([P, 128 * EARLY], U8, name="xqs%d" % g, align_bytes=64)
             nc.vector.quantize_mx(out=xq[g][:].bitcast(FP8X4), scales=xqs[g][:], in_=xint[g][:])
 
-        ww, wint, wq, wqs = {}, {}, {}, {}
+        ww, wint, wq, wqs, wbank = {}, {}, {}, {}, {}
 
-        def w_widen(u):
+        def w_widen(u, parts=1):
             if u % PASSES < SPLIT_PASSES:
                 tile = wide.tile([P, 2048], BF16, name="wide_unit")
                 ww[u] = tile[:].rearrange("p (t n) -> p t n", t=4)
@@ -158,20 +181,42 @@ def tile_patch_embed_qkv_d4_kernel(tc, x_bytes, x_scale, w_bytes, w_scale, gain,
                 tile = wide.tile([P, 4096], BF16, name="wide_pass")
                 both = tile[:].rearrange("p (t n) -> p t n", t=4)
                 ww[u], ww[u + PASSES] = both[:, :, 0:512], both[:, :, 512:1024]
-            nc.scalar.copy(out=tile[:], in_=wb[u][:].bitcast(FP8))
+            n = tile.shape[1] // parts
+            for j in range(parts):
+                nc.scalar.copy(out=tile[:, n * j:n * j + n], in_=wb[u][:, n * j:n * j + n].bitcast(FP8))
 
-        def w_weave(u, b, on_scalar):
-            half, g = divmod(u, PASSES)
+        def w_int(u, on_scalar):
             if u not in wint:
                 wint[u] = stage.tile([P, 2048], BF16, name="wint_s" if on_scalar else "wint_v", align_bytes=64)
+            return wint[u]
+
+        def w_scale_col(u, b):
+            half, g = divmod(u, PASSES)
+            col = 32 * g + 4 * half + b
+            return wsc[:, col:col + 1]
+
+        def w_weave(u, b, on_scalar):
             walk = "p b m t j" if on_scalar else "p b m j t"
             src = ww[u].rearrange("p j (b m t) -> " + walk, b=4, t=4)[:, b]
-            dst = wint[u][:].rearrange("p (t b m j) -> " + walk, t=4, b=4, j=4)[:, b]
-            col = 8 * g + 4 * half + b
+            dst = w_int(u, on_scalar)[:].rearrange("p (t b m j) -> " + walk, t=4, b=4, j=4)[:, b]
             if on_scalar:
-                nc.scalar.activation(out=dst, in_=src, func=COPY, scale=wsc[:, col:col + 1])
+                nc.scalar.activation(out=dst, in_=src, func=COPY, scale=w_scale_col(u, b))
             else:
-                nc.vector.tensor_scalar(out=dst, in0=src, scalar1=wsc[:, col:col + 1], scalar2=None, op0=MULT)
+                nc.vector.tensor_scalar(out=dst, in0=src, scalar1=w_scale_col(u, b), scalar2=None, op0=MULT)
+
+        def w_lay(u, blocks):
+            tile = next_bank(BF16)
+            for n, b in enumerate(blocks):
+                wbank[u, b] = tile[:, 512 * n:512 * n + 512]
+                nc.tensor.matmul(
+                    wbank[u, b].rearrange("p (t m j) -> p m t j", t=4, j=4), lhsT=ident_b[:],
+                    rhs=ww[u][:, :, 128 * b:128 * b + 128].rearrange("p j (m t) -> p m t j", t=4), start=True, stop=True)
+
+        def w_exit(u, blocks):
+            for b in blocks:
+                nc.vector.tensor_scalar(
+                    out=w_int(u, False)[:].rearrange("p (t b c) -> p b t c", t=4, b=4)[:, b],
+                    in0=wbank[u, b].rearrange("p (t c) -> p t c", t=4), scalar1=w_scale_col(u, b), scalar2=None, op0=MULT)
 
         def w_quant(u, parts=1):
             wq[u] = stage.tile([P, 512], U32, name="wq", align_bytes=64)
@@ -181,31 +226,37 @@ def tile_patch_embed_qkv_d4_kernel(tc, x_bytes, x_scale, w_bytes, w_scale, gain,
                 nc.vector.quantize_mx(
                     out=wq[u][:, n * j:n * j + n].bitcast(FP8X4), scales=wqs[u][:, n * j:n * j + n], in_=wint[u][:, 4 * n * j:4 * n * (j + 1)])
 
-        e = {}
+        e, ebank = {}, {}
 
-        def product_1(u, first, last, slices=range(4)):
+        def mm1(dst, u, t, rhs, rhs_scale, start, stop):
+            cols = slice(128 * t, 128 * t + 128)
+            nc.tensor.matmul_mx(out=dst, lhsT=wq[u][:, cols].bitcast(FP8X4), lhsT_scale=wqs[u][:, cols],
+                                rhs=rhs.bitcast(FP8X4), rhs_scale=rhs_scale, start=start, stop=stop)
+
+        def open_sums(half):
+            for n in range(4):
+                ebank[half, n] = hold_bank((half, n))
+
+        def product_1(u, first, last, images=range(2)):
             half, g = divmod(u, PASSES)
-            for a in range(1 + half):
-                for t in slices:
-                    cols = slice(128 * t, 128 * t + 128)
-                    if half == 0:
-                        if first:
-                            e[0, t] = bank(t)
-                        toks, dst, start, stop = slice(0, TOK), e[0, t][:], first, last
-                    else:
-                        if first and t % 2 == 0:
-                            e[1, t // 2, a] = bank(4 + 2 * a + t // 2)
-                        toks, dst = slice(IMAGE * a, IMAGE * a + IMAGE), e[1, t // 2, a][:, IMAGE * (t % 2):IMAGE * (t % 2) + IMAGE]
-                        start, stop = first and t % 2 == 0, last and t % 2 == 1
-                    nc.tensor.matmul_mx(
-                        out=dst, lhsT=wq[u][:, cols].bitcast(FP8X4), lhsT_scale=wqs[u][:, cols],
-                        rhs=xq[g][:, toks].bitcast(FP8X4), rhs_scale=xqs[g][:, toks], start=start, stop=stop)
+            if 0 in images:
+                for t in range(4):
+                    dst = ebank[half, t // 2][:, IMAGE * (t % 2):IMAGE * (t % 2) + IMAGE]
+                    e[half, t, 0] = dst
+                    mm1(dst, u, t, xq[g][:, 0:IMAGE], xqs[g][:, 0:IMAGE], first and t % 2 == 0, last and t % 2 == 1)
+            for j in (2, 3):
+                if j in images or 1 in images:
+                    toks = slice(128 * j, 128 * j + 128)
+                    for t in range(4):
+                        dst = ebank[half, j][:, 128 * t:128 * t + 128]
+                        e[half, t, j] = dst
+                        mm1(dst, u, t, xq[g][:, toks], xqs[g][:, toks], first and t == 0, last and t == 3)
 
         pos_t = keep.tile([P, 2048], BF16, name="pos_t")
         pos_bank = {}
 
         def pos_turn(half):
-            pos_bank[half] = bank(4 + half)
+            pos_bank[half] = next_bank()
             words = pos_sb[:].bitcast(F32)
             for u in range(2):
                 for i in range(2):
@@ -217,38 +268,50 @@ def tile_patch_embed_qkv_d4_kernel(tc, x_bytes, x_scale, w_bytes, w_scale, gain,
             nc.scalar.copy(out=pos_t[:, 1024 * half:1024 * half + 1024].bitcast(F32), in_=pos_bank[half][:])
 
         hs = [keep.tile([P, 4 * TOK], BF16, name="hs%d" % h) for h in range(2)]
-        hint = [keep.tile([P, 4 * TOK], BF16, name="hint%d" % h, align_bytes=64) for h in range(2)]
+        hint, h32 = {}, {}
         hq = [keep.tile([P, TOK], U32, name="hq%d" % h, align_bytes=64) for h in range(2)]
         hqs = [keep.tile([P, TOK], U8, name="hqs%d" % h, align_bytes=64) for h in range(2)]
 
-        def h_add(half, lo, hi, slices=range(4)):
+        def h_add(half, j, n=1, slices=range(4)):
+            lo, hi = 128 * j, 128 * (j + n)
             r = lo % IMAGE
             for t in slices:
                 at = 1024 * half + 2 * IMAGE * (t // 2) + 2 * r + t % 2
-                if half == 0:
-                    src = e[0, t][:, lo:hi]
-                else:
-                    src = e[1, t // 2, lo // IMAGE][:, IMAGE * (t % 2) + r:IMAGE * (t % 2) + r + hi - lo]
+                src = e[half, t, 0][:, lo:hi] if j < 2 else e[half, t, j]
                 nc.vector.scalar_tensor_tensor(
                     out=hs[half][:, TOK * t + lo:TOK * t + hi], in0=src,
                     scalar=gain_f[:, 4 * half + t:4 * half + t + 1], in1=pos_t[:, at:at + 2 * (hi - lo) - 1:2], op0=MULT, op1=ADD)
 
-        def h_weave(half, i, n=1, copy=nc.scalar.copy):
-            copy(
-                out=hint[half][:, 512 * i:512 * (i + n)].rearrange("p (r t) -> p r t", t=4),
-                in_=hs[half][:].rearrange("p (t r) -> p r t", t=4)[:, 128 * i:128 * (i + n)])
+        def h_int(half, j):
+            hint[half, j] = keep.tile([P, 512], BF16, name="hint%d%d" % (half, min(j, 2)), align_bytes=64)
+            return hint[half, j][:]
 
-        def h_quant(half, i, n=1):
-            toks = slice(128 * i, 128 * (i + n))
-            nc.vector.quantize_mx(
-                out=hq[half][:, toks].bitcast(FP8X4), scales=hqs[half][:, toks], in_=hint[half][:, 512 * i:512 * (i + n)])
+        def h_weave(half, j, copy=nc.scalar.copy):
+            copy(
+                out=h_int(half, j).rearrange("p (r t) -> p r t", t=4),
+                in_=hs[half][:].rearrange("p (t r) -> p r t", t=4)[:, 128 * j:128 * j + 128])
+
+        def h_gain(half, j):
+            h32[half] = keep.tile([P, 512], F32, name="h32%d" % half)
+            for t in range(4):
+                nc.scalar.activation(out=h32[half][:, 128 * t:128 * t + 128], in_=e[half, t, j], func=COPY, scale=gain_f[:, 4 * half + t:4 * half + t + 1])
+
+        def h_pos(half, j):
+            nc.gpsimd.tensor_tensor(
+                out=h_int(half, j).rearrange("p (r u e) -> p r u e", u=2, e=2),
+                in0=h32[half][:].rearrange("p (u e r) -> p r u e", u=2, e=2),
+                in1=pos_t[:].rearrange("p (h u i r e) -> p h i r u e", h=2, u=2, i=2, e=2)[:, half, j % 2], op=ADD)
+
+        def h_quant(half, j):
+            toks = slice(128 * j, 128 * j + 128)
+            nc.vector.quantize_mx(out=hq[half][:, toks].bitcast(FP8X4), scales=hqs[half][:, toks], in_=hint[half, j][:])
 
         ob, ot = {}, {}
 
         def product_2(n, halves=range(2)):
             i, c = divmod(n, COLUMN_BLOCKS)
             if n not in ob:
-                ob[n] = bank(n % 8)
+                ob[n] = next_bank()
             toks = slice(128 * i, 128 * i + 128)
             for h in halves:
                 nc.tensor.matmul_mx(
@@ -257,126 +320,177 @@ def tile_patch_embed_qkv_d4_kernel(tc, x_bytes, x_scale, w_bytes, w_scale, gain,
                     rhs=vw[h][:, 1024 * c:1024 * c + 1024].bitcast(FP4X4), rhs_scale=vs[:, N * h + 512 * c:N * h + 512 * c + 512],
                     start=(h == 0), stop=(h == 1))
 
+        waiting = []
+
+        def store(i, first, width, queue):
+            rows = out.rearrange("(a p i) n -> a i p n", a=2, i=2)[i // 2, i % 2]
+            queue.dma_start(out=rows[:, first:first + width], in_=ot[i, first][:, 0:width])
+
         def finish(n):
             i, c = divmod(n, COLUMN_BLOCKS)
-            rows = out.rearrange("(a p i) n -> a i p n", a=2, i=2)[i // 2, i % 2]
             first = 0
             for width in STORES[i]:
-                lo, hi = max(first, 512 * c), min(first + width, 512 * c + 512)
-                if lo < hi:
-                    if lo == first:
-                        ot[i, first] = wide.tile([P, 1024], F32, name="wide_unit" if len(ot) % 2 else "wide_pass")
-                    o = ot[i, first]
-                    nc.vector.tensor_tensor(out=o[:, lo - first:hi - first], in0=ob[n][:, lo - 512 * c:hi - 512 * c], in1=bias_sb[:, lo:hi], op=ADD)
-                    if hi == first + width:
-                        queue = nc.scalar if i > 0 and first // 1024 % 2 == i % 2 else nc.sync
-                        queue.dma_start(out=rows[:, first:hi], in_=o[:, 0:width])
+                if first <= 512 * c < first + width:
+                    if 512 * c == first:
+                        ot[i, first] = wide.tile([P, width], F32, name="wide_pass" if width > 1024 or len(ot) % 2 == 0 else "wide_unit")
+                    o = ot[i, first][:, 512 * c - first:512 * c - first + 512]
+                    cols = slice(512 * c, 512 * c + 512)
+                    if n in GPSIMD_TILES:
+                        nc.scalar.copy(out=o, in_=ob[n][:])
+                        nc.gpsimd.tensor_tensor(out=o, in0=o, in1=bias_sb[:, cols], op=ADD)
+                    else:
+                        nc.vector.tensor_tensor(out=o, in0=ob[n][:], in1=bias_sb[:, cols], op=ADD)
+                    if 512 * c + 512 == first + width:
+                        if n in GPSIMD_TILES:
+                            waiting.append((i, first, width))
+                        else:
+                            store(i, first, width, nc.scalar if n in SCALAR_STORES else nc.sync)
                 first = first + width
 
-        nc.scalar.activation(out=gain_f[:], in_=gain_b[:], func=COPY)
-        for i in range(2):
-            for g in range(2):
-                x_widen(g, 0, range(i, i + 1))
-        x_turn(0, 0)
-        x_turn(1, 0)
-        w_widen(0)
-        for i in range(2):
-            for g in range(2):
-                x_widen(g, 1, range(i, i + 1))
-        x_turn(0, 1)
-        x_turn(1, 1)
-        pick_w_scales()
-        w_widen(1)
-        x_out(0, 0)
-        x_out(0, 1)
         blocks = [(u, b) for u in HALF_1 for b in range(4)]
-        scalar_blocks, vector_blocks = blocks[:SCALAR_BLOCKS], blocks[SCALAR_BLOCKS:]
+        scalar_blocks = blocks[:SCALAR_BLOCKS]
         shared = scalar_blocks[-1][0]
         scalar_units = list(HALF_1[:list(HALF_1).index(shared)])
         vector_units = list(range(PASSES)) + list(reversed(HALF_1[list(HALF_1).index(shared):]))
+        laid = {u: list(range(4 - n, 4)) for u, n in zip(vector_units, LAID)}
+        theirs = list(scalar_blocks)
+
+        def lay(u):
+            bs = laid.get(u, [])
+            for n in range(0, len(bs), 2):
+                w_lay(u, bs[n:n + 2])
 
         def vector_weave(u):
             for b in range(4):
-                if u < PASSES or (u, b) in vector_blocks:
+                if (u, b) not in theirs and b not in laid.get(u, []):
                     w_weave(u, b, False)
+            w_exit(u, laid.get(u, []))
 
         def scalar_weave(n):
             for j in range(min(n, len(scalar_blocks))):
                 w_weave(*scalar_blocks.pop(0), True)
 
+        open_sums(0)
+        nc.scalar.activation(out=gain_f[:], in_=gain_b[:], func=COPY)
+        for j in range(2):
+            for g in range(2):
+                x_widen(g, [j])
+        x_turn(0, [0, 1])
+        w_widen(0, 2)
+        for j in range(2, 4):
+            for g in range(2):
+                x_widen(g, [j])
+        x_turn(0, [2, 3])
+        x_turn(1, [0, 1])
+        x_out(0, [0, 1])
+        w_widen(1)
+        x_out(0, [2, 3])
         vector_weave(0)
+        lay(1)
+        x_turn(1, [2, 3])
         for s in range(PASSES):
-            if s + 2 < PASSES:
-                for a in range(2):
-                    x_widen(s + 2, a)
-                    x_turn(s + 2, a)
-            if s > 0:
-                product_1(s - 1, s == 1, False, range(2, 4))
+            if s + 1 < PASSES and s < 4:
+                x_out(s + 1, [0, 1])
+                x_out(s + 1, [2, 3])
             if s + 2 < PASSES:
                 w_widen(s + 2)
-            if s + 1 < PASSES:
-                x_out(s + 1, 0)
-                x_out(s + 1, 1)
+            if s in EXTRA:
+                scalar_weave(1)
+            if s == 4:
+                x_out(s + 1, [0, 1])
+                x_out(s + 1, [2, 3])
+            if s + 2 < PASSES:
+                x_widen(s + 2, range(4))
+            if s > 0:
+                product_1(s - 1, s == 1, False, [1])
+            vector_weave(vector_units[s + 1])
+            if s + 2 < PASSES:
+                x_turn(s + 2, [0, 1])
+            lay(vector_units[s + 2])
+            if s + 2 < PASSES:
+                x_turn(s + 2, [2, 3])
             if s + 3 == PASSES:
                 pos_turn(0)
-                pos_turn(1)
                 w_widen(PASSES)
             if s + 2 == PASSES:
                 scalar_weave(2)
                 pos_out(0)
-                pos_out(1)
-                scalar_weave(2)
+                scalar_weave(2 - len(EXTRA))
                 w_widen(PASSES + 1)
                 scalar_weave(len(scalar_blocks))
-            vector_weave(vector_units[s + 1])
             x_quant(s)
             w_quant(s)
-            product_1(s, s == 0, s == PASSES - 1, range(0, 2) if s + 1 < PASSES else range(4))
+            product_1(s, s == 0, s == PASSES - 1, [0] if s + 1 < PASSES else [0, 1])
+
+        open_sums(1)
 
         def quant_and_multiply(u, first=False):
             w_quant(u)
             product_1(u, first, False)
 
         quant_and_multiply(vector_units[PASSES], True)
-        between = [range(0, 2), range(2, 4)]
-        for u in vector_units[PASSES + 1:]:
+        for n, u in enumerate(vector_units[PASSES + 1:]):
             vector_weave(u)
-            if scalar_units:
-                quant_and_multiply(scalar_units.pop(0))
-            if u != shared:
-                quant_and_multiply(u)
-            if between:
-                h_add(0, 0, IMAGE, between.pop(0))
-        for u in scalar_units:
+            if u == shared:
+                break
+            quant_and_multiply(scalar_units.pop(0))
+            if n == 0:
+                h_add(0, 0, 2, range(0, 2))
+                free_bank((0, 0))
+                pos_turn(1)
             quant_and_multiply(u)
-        h_weave(0, 0, 2)
-        h_add(0, IMAGE, TOK, range(0, 1))
+        for n, u in enumerate(scalar_units):
+            w_quant(u)
+            product_1(u, False, False, [0])
+            if n == 0:
+                h_add(0, 0, 1, range(2, 4))
+        pos_out(1)
+        h_weave(0, 0)
         w_quant(shared, 2)
-        product_1(shared, False, True)
-
-        h_add(0, IMAGE, TOK, range(1, 4))
-        h_add(1, 0, 128)
-        h_quant(0, 0, 2)
+        product_1(shared, False, True, [0])
+        last_units = scalar_units + [shared]
+        for u in last_units:
+            product_1(u, False, u == shared, [2])
+        h_add(0, 1, 1, range(2, 4))
+        free_bank((0, 1))
+        h_weave(0, 1)
+        h_add(0, 2)
+        free_bank((0, 2))
+        h_add(1, 0)
+        h_quant(0, 0)
         h_weave(1, 0, copy=nc.vector.tensor_copy)
         for n in range(3):
             product_2(n, range(0, 1))
-        h_add(1, 128, IMAGE, range(0, 2))
+        h_add(1, 1, 1, range(0, 2))
         h_quant(1, 0)
-        h_add(1, 128, IMAGE, range(2, 4))
+        h_add(1, 1, 1, range(2, 4))
+        free_bank((1, 0))
+        free_bank((1, 1))
+        h_weave(0, 2)
         h_weave(1, 1)
-        h_add(1, IMAGE, TOK, range(0, 2))
+        h_add(1, 2)
+        free_bank((1, 2))
+        h_weave(1, 2)
         for n in range(3):
             product_2(n, range(1, 2))
+        for u in last_units:
+            product_1(u, False, u == shared, [3])
         product_2(3)
         for n in range(TOKEN_TILES * COLUMN_BLOCKS):
             finish(n)
             if n == 0:
-                h_add(1, IMAGE, TOK, range(2, 4))
+                h_quant(0, 1)
                 h_quant(1, 1)
-                h_weave(0, 2, 2)
-                h_weave(1, 2, 2)
-            if n == 7:
-                h_quant(0, 2, 2)
-                h_quant(1, 2, 2)
+                for h in range(2):
+                    h_gain(h, 3)
+                    free_bank((h, 3))
+            if n == Q2:
+                h_quant(1, 2)
+                h_quant(0, 2)
+                h_pos(0, 3)
+                h_pos(1, 3)
+            if n == Q3:
+                h_quant(0, 3)
+                h_quant(1, 3)
             if n + 4 < TOKEN_TILES * COLUMN_BLOCKS:
                 product_2(n + 4)

@@ -26,15 +26,17 @@ COLUMN_BLOCKS = N // 512
 FLOPS = 2 * TOK * K * D + 2 * TOK * D * N
 
 EARLY = 4
-SCALAR_BLOCKS = 13
-LAID = ()
+SCALAR_BLOCKS = 12
+LAID = (0, 0, 2, 2, 2, 2, 2)
 SPLIT_PASSES = 2
-EXTRA = (1,)
+EXTRA = (3,)
 HALF_1 = (8, 6, 7, 9, 10, 11)
 GPSIMD_TILES = ()
 SCALAR_STORES = (15, 19, 22)
 LATE_STORE = 7
-Q2 = 3
+Q2 = 5
+PARTS = 4
+HINT_PLACE = ((0, 1, 3, 3), (2, 3, 4, 4))
 Q3 = 13
 STORES = ((512, 512, 1024, 1024), (1024, 1024, 1024), (1024, 1024, 1024), (1024, 1024, 512, 512))
 
@@ -53,10 +55,12 @@ def tile_patch_embed_qkv_d4_kernel(tc, x_bytes, x_scale, w_bytes, w_scale, gain,
 
         ring = list(range(8))
 
-        def next_bank(dtype=F32):
+        def next_bank(dtype=F32, ring=ring):
             b = ring.pop(0)
             ring.append(b)
             return bank(b, dtype)
+
+        x_ring, w_ring = [4, 5, 6, 7], [6, 7]
 
         held = {}
 
@@ -70,8 +74,7 @@ def tile_patch_embed_qkv_d4_kernel(tc, x_bytes, x_scale, w_bytes, w_scale, gain,
         ident = keep.tile([P, P], F32, name="ident")
         make_identity(nc, ident[:])
         ident_b = keep.tile([P, P], BF16, name="ident_b")
-        if LAID:
-            make_identity(nc, ident_b[:])
+        make_identity(nc, ident_b[:])
 
         xs = keep.tile([P, TOKEN_TILES * 24], F32, name="xs")
         nc.scalar.dma_start(out=xs[:].rearrange("p (a c) -> p a c", a=2), in_=x_scale.rearrange("(a p i) c -> p a (i c)", a=2, i=2))
@@ -151,7 +154,7 @@ def tile_patch_embed_qkv_d4_kernel(tc, x_bytes, x_scale, w_bytes, w_scale, gain,
 
         def x_turn(g, tiles):
             words = xw[g][:].bitcast(F32)
-            xbank[g, tiles[0]] = next_bank()
+            xbank[g, tiles[0]] = next_bank(F32, x_ring)
             for n, j in enumerate(tiles):
                 for u in range(2):
                     first = 256 * j + 128 * u
@@ -205,7 +208,7 @@ def tile_patch_embed_qkv_d4_kernel(tc, x_bytes, x_scale, w_bytes, w_scale, gain,
                 nc.vector.tensor_scalar(out=dst, in0=src, scalar1=w_scale_col(u, b), scalar2=None, op0=MULT)
 
         def w_lay(u, blocks):
-            tile = next_bank(BF16)
+            tile = next_bank(BF16, w_ring)
             for n, b in enumerate(blocks):
                 wbank[u, b] = tile[:, 512 * n:512 * n + 512]
                 nc.tensor.matmul(
@@ -256,7 +259,7 @@ def tile_patch_embed_qkv_d4_kernel(tc, x_bytes, x_scale, w_bytes, w_scale, gain,
         pos_bank = {}
 
         def pos_turn(half):
-            pos_bank[half] = next_bank()
+            pos_bank[half] = next_bank(F32, ring if half else x_ring)
             words = pos_sb[:].bitcast(F32)
             for u in range(2):
                 for i in range(2):
@@ -283,7 +286,7 @@ def tile_patch_embed_qkv_d4_kernel(tc, x_bytes, x_scale, w_bytes, w_scale, gain,
                     scalar=gain_f[:, 4 * half + t:4 * half + t + 1], in1=pos_t[:, at:at + 2 * (hi - lo) - 1:2], op0=MULT, op1=ADD)
 
         def h_int(half, j):
-            hint[half, j] = keep.tile([P, 512], BF16, name="hint%d%d" % (half, min(j, 2)), align_bytes=64)
+            hint[half, j] = keep.tile([P, 512], BF16, name="hint%d" % HINT_PLACE[half][j], align_bytes=64)
             return hint[half, j][:]
 
         def h_weave(half, j, copy=nc.scalar.copy):
@@ -292,14 +295,14 @@ def tile_patch_embed_qkv_d4_kernel(tc, x_bytes, x_scale, w_bytes, w_scale, gain,
                 in_=hs[half][:].rearrange("p (t r) -> p r t", t=4)[:, 128 * j:128 * j + 128])
 
         def h_gain(half, j):
-            h32[half] = keep.tile([P, 512], F32, name="h32%d" % half)
+            h32[half, j] = keep.tile([P, 512], F32, name="h32%d%d" % (half, j))
             for t in range(4):
-                nc.scalar.activation(out=h32[half][:, 128 * t:128 * t + 128], in_=e[half, t, j], func=COPY, scale=gain_f[:, 4 * half + t:4 * half + t + 1])
+                nc.scalar.activation(out=h32[half, j][:, 128 * t:128 * t + 128], in_=e[half, t, j], func=COPY, scale=gain_f[:, 4 * half + t:4 * half + t + 1])
 
         def h_pos(half, j):
             nc.gpsimd.tensor_tensor(
                 out=h_int(half, j).rearrange("p (r u e) -> p r u e", u=2, e=2),
-                in0=h32[half][:].rearrange("p (u e r) -> p r u e", u=2, e=2),
+                in0=h32[half, j][:].rearrange("p (u e r) -> p r u e", u=2, e=2),
                 in1=pos_t[:].rearrange("p (h u i r e) -> p h i r u e", h=2, u=2, i=2, e=2)[:, half, j % 2], op=ADD)
 
         def h_quant(half, j):
@@ -364,7 +367,6 @@ def tile_patch_embed_qkv_d4_kernel(tc, x_bytes, x_scale, w_bytes, w_scale, gain,
             for b in range(4):
                 if (u, b) not in theirs and b not in laid.get(u, []):
                     w_weave(u, b, False)
-            w_exit(u, laid.get(u, []))
 
         def scalar_weave(n):
             for j in range(min(n, len(scalar_blocks))):
@@ -385,78 +387,89 @@ def tile_patch_embed_qkv_d4_kernel(tc, x_bytes, x_scale, w_bytes, w_scale, gain,
         x_out(0, [0, 1])
         w_widen(1)
         x_out(0, [2, 3])
-        vector_weave(0)
-        lay(1)
         x_turn(1, [2, 3])
+        x_ring.remove(6)
+        x_ring.remove(7)
+        vector_weave(0)
         for s in range(PASSES):
-            if s + 1 < PASSES and s < 4:
+            u = vector_units[s + 1]
+            if s + 1 < PASSES:
                 x_out(s + 1, [0, 1])
                 x_out(s + 1, [2, 3])
             if s + 2 < PASSES:
                 w_widen(s + 2)
+                x_widen(s + 2, range(4))
             if s in EXTRA:
                 scalar_weave(1)
-            if s == 4:
-                x_out(s + 1, [0, 1])
-                x_out(s + 1, [2, 3])
-            if s + 2 < PASSES:
-                x_widen(s + 2, range(4))
             if s > 0:
-                product_1(s - 1, s == 1, False, [1])
-            vector_weave(vector_units[s + 1])
+                product_1(s - 1, s == 1, False, [0])
             if s + 2 < PASSES:
+                vector_weave(u)
                 x_turn(s + 2, [0, 1])
-            lay(vector_units[s + 2])
-            if s + 2 < PASSES:
                 x_turn(s + 2, [2, 3])
-            if s + 3 == PASSES:
+            if s + 2 == PASSES:
                 pos_turn(0)
                 w_widen(PASSES)
-            if s + 2 == PASSES:
-                scalar_weave(2)
                 pos_out(0)
-                scalar_weave(2 - len(EXTRA))
+                scalar_weave(4 - len(EXTRA))
                 w_widen(PASSES + 1)
                 scalar_weave(len(scalar_blocks))
+            if s > 0:
+                product_1(s - 1, s == 1, False, [1])
             x_quant(s)
-            w_quant(s)
-            product_1(s, s == 0, s == PASSES - 1, [0] if s + 1 < PASSES else [0, 1])
+            if s + 2 < PASSES:
+                w_exit(u, laid.get(u, []))
+                w_quant(s)
+            else:
+                w_quant(s)
+                vector_weave(u)
+                w_exit(u, laid.get(u, []))
+            lay(vector_units[s + 2])
+        product_1(PASSES - 1, False, True)
 
         open_sums(1)
 
-        def quant_and_multiply(u, first=False):
-            w_quant(u)
-            product_1(u, first, False)
+        done, last_units = [], []
 
-        quant_and_multiply(vector_units[PASSES], True)
-        for n, u in enumerate(vector_units[PASSES + 1:]):
+        def quant_and_multiply(u):
+            w_quant(u, PARTS if u == shared else 1)
+            if len(done) < 3:
+                product_1(u, not done, False)
+            else:
+                product_1(u, False, u == shared, [0])
+                last_units.append(u)
+            done.append(u)
+
+        rest = vector_units[PASSES:]
+        for n, u in enumerate(rest[1:]):
+            if n == 0:
+                w_weave(u, 0, False)
+                quant_and_multiply(rest[0])
+                theirs.append((u, 0))
             vector_weave(u)
-            if u == shared:
-                break
-            quant_and_multiply(scalar_units.pop(0))
+            if scalar_units:
+                quant_and_multiply(scalar_units.pop(0))
             if n == 0:
                 h_add(0, 0, 2, range(0, 2))
                 free_bank((0, 0))
                 pos_turn(1)
+            if u != shared:
+                quant_and_multiply(u)
+        for u in scalar_units:
             quant_and_multiply(u)
-        for n, u in enumerate(scalar_units):
-            w_quant(u)
-            product_1(u, False, False, [0])
-            if n == 0:
-                h_add(0, 0, 1, range(2, 4))
+        h_add(0, 0, 1, range(2, 4))
         pos_out(1)
         h_weave(0, 0)
-        w_quant(shared, 2)
-        product_1(shared, False, True, [0])
-        last_units = scalar_units + [shared]
+        quant_and_multiply(shared)
         for u in last_units:
             product_1(u, False, u == shared, [2])
+        h_gain(0, 2)
+        free_bank((0, 2))
         h_add(0, 1, 1, range(2, 4))
         free_bank((0, 1))
         h_weave(0, 1)
-        h_add(0, 2)
-        free_bank((0, 2))
-        h_add(1, 0)
+        h_add(1, 0, 1, range(0, 2))
+        h_add(1, 0, 1, range(2, 4))
         h_quant(0, 0)
         h_weave(1, 0, copy=nc.vector.tensor_copy)
         for n in range(3):
@@ -466,7 +479,6 @@ def tile_patch_embed_qkv_d4_kernel(tc, x_bytes, x_scale, w_bytes, w_scale, gain,
         h_add(1, 1, 1, range(2, 4))
         free_bank((1, 0))
         free_bank((1, 1))
-        h_weave(0, 2)
         h_weave(1, 1)
         h_add(1, 2)
         free_bank((1, 2))
@@ -481,6 +493,7 @@ def tile_patch_embed_qkv_d4_kernel(tc, x_bytes, x_scale, w_bytes, w_scale, gain,
             if n == 0:
                 h_quant(0, 1)
                 h_quant(1, 1)
+                h_pos(0, 2)
                 for h in range(2):
                     h_gain(h, 3)
                     free_bank((h, 3))

@@ -34,10 +34,10 @@ HALF_1 = (8, 6, 7, 9, 10, 11)
 GPSIMD_TILES = ()
 SCALAR_STORES = (15, 19, 22)
 LATE_STORE = 7
-Q2 = 5
+Q2 = 3
 PARTS = 4
-HINT_PLACE = ((0, 1, 3, 3), (2, 3, 4, 4))
-Q3 = 13
+HINT_PLACE = ((0, 1, 2, 2), (2, 3, 4, 4))
+Q3 = 15
 STORES = ((512, 512, 1024, 1024), (1024, 1024, 1024), (1024, 1024, 1024), (1024, 1024, 512, 512))
 
 
@@ -69,7 +69,7 @@ def tile_patch_embed_qkv_d4_kernel(tc, x_bytes, x_scale, w_bytes, w_scale, gain,
             return bank(held[key])
 
         def free_bank(key):
-            ring.append(held.pop(key))
+            ring.insert(0, held.pop(key))
 
         ident = keep.tile([P, P], F32, name="ident")
         make_identity(nc, ident[:])
@@ -476,34 +476,40 @@ def tile_patch_embed_qkv_d4_kernel(tc, x_bytes, x_scale, w_bytes, w_scale, gain,
             product_2(n, range(0, 1))
         h_add(1, 1, 1, range(0, 2))
         h_quant(1, 0)
+        h_pos(0, 2)
         h_add(1, 1, 1, range(2, 4))
-        free_bank((1, 0))
-        free_bank((1, 1))
         h_weave(1, 1)
         h_add(1, 2)
-        free_bank((1, 2))
+        for n in (2, 1, 0):
+            free_bank((1, n))
         h_weave(1, 2)
         for n in range(3):
             product_2(n, range(1, 2))
+        for n in range(3, COLUMN_BLOCKS):
+            product_2(n)
         for u in last_units:
             product_1(u, False, u == shared, [3])
-        product_2(3)
+        issued = COLUMN_BLOCKS
+        ready = COLUMN_BLOCKS
         for n in range(TOKEN_TILES * COLUMN_BLOCKS):
             finish(n)
             if n == 0:
-                h_quant(0, 1)
-                h_quant(1, 1)
-                h_pos(0, 2)
                 for h in range(2):
                     h_gain(h, 3)
-                    free_bank((h, 3))
             if n == Q2:
-                h_quant(1, 2)
-                h_quant(0, 2)
+                for j in (1, 2):
+                    h_quant(1, j)
+                    h_quant(0, j)
                 h_pos(0, 3)
                 h_pos(1, 3)
+                ready = 3 * COLUMN_BLOCKS
+            if n == COLUMN_BLOCKS:
+                free_bank((0, 3))
+                free_bank((1, 3))
             if n == Q3:
                 h_quant(0, 3)
                 h_quant(1, 3)
-            if n + 4 < TOKEN_TILES * COLUMN_BLOCKS:
-                product_2(n + 4)
+                ready = 4 * COLUMN_BLOCKS
+            for m in range(issued, min(n + 5, ready)):
+                product_2(m)
+            issued = max(issued, min(n + 5, ready))

@@ -34,10 +34,11 @@ HALF_1 = (8, 6, 7, 9, 10, 11)
 GPSIMD_TILES = ()
 SCALAR_STORES = (15, 19, 22)
 LATE_STORE = 7
-Q2 = 3
+Q1 = 1
+Q2 = 8
 PARTS = 4
-HINT_PLACE = ((0, 1, 2, 2), (2, 3, 4, 4))
-Q3 = 15
+SUM_PLACE = {(0, 2): "hint10", (1, 2): "hint11", (1, 3): "hint12"}
+Q3 = 14
 STORES = ((512, 512, 1024, 1024), (1024, 1024, 1024), (1024, 1024, 1024), (1024, 1024, 512, 512))
 
 
@@ -271,7 +272,7 @@ def tile_patch_embed_qkv_d4_kernel(tc, x_bytes, x_scale, w_bytes, w_scale, gain,
             nc.scalar.copy(out=pos_t[:, 1024 * half:1024 * half + 1024].bitcast(F32), in_=pos_bank[half][:])
 
         hs = [keep.tile([P, 4 * TOK], BF16, name="hs%d" % h) for h in range(2)]
-        hint, h32 = {}, {}
+        hint, h32, hsum = {}, {}, {}
         hq = [keep.tile([P, TOK], U32, name="hq%d" % h, align_bytes=64) for h in range(2)]
         hqs = [keep.tile([P, TOK], U8, name="hqs%d" % h, align_bytes=64) for h in range(2)]
 
@@ -286,7 +287,7 @@ def tile_patch_embed_qkv_d4_kernel(tc, x_bytes, x_scale, w_bytes, w_scale, gain,
                     scalar=gain_f[:, 4 * half + t:4 * half + t + 1], in1=pos_t[:, at:at + 2 * (hi - lo) - 1:2], op0=MULT, op1=ADD)
 
         def h_int(half, j):
-            hint[half, j] = keep.tile([P, 512], BF16, name="hint%d" % HINT_PLACE[half][j], align_bytes=64)
+            hint[half, j] = keep.tile([P, 512], BF16, name="hint%d%d" % (half, j), align_bytes=64)
             return hint[half, j][:]
 
         def h_weave(half, j, copy=nc.scalar.copy):
@@ -300,10 +301,14 @@ def tile_patch_embed_qkv_d4_kernel(tc, x_bytes, x_scale, w_bytes, w_scale, gain,
                 nc.scalar.activation(out=h32[half, j][:, 128 * t:128 * t + 128], in_=e[half, t, j], func=COPY, scale=gain_f[:, 4 * half + t:4 * half + t + 1])
 
         def h_pos(half, j):
+            hsum[half, j] = keep.tile([P, 512], BF16, name=SUM_PLACE.get((half, j), "hsum%d%d" % (half, j)), align_bytes=64)
             nc.gpsimd.tensor_tensor(
-                out=h_int(half, j).rearrange("p (r u e) -> p r u e", u=2, e=2),
-                in0=h32[half, j][:].rearrange("p (u e r) -> p r u e", u=2, e=2),
-                in1=pos_t[:].rearrange("p (h u i r e) -> p h i r u e", h=2, u=2, i=2, e=2)[:, half, j % 2], op=ADD)
+                out=hsum[half, j][:].rearrange("p (u e r) -> p u e r", u=2, e=2),
+                in0=h32[half, j][:].rearrange("p (u e r) -> p u e r", u=2, e=2),
+                in1=pos_t[:].rearrange("p (h u i r e) -> p h i u e r", h=2, u=2, i=2, e=2)[:, half, j % 2], op=ADD)
+
+        def h_weave_sum(half, j):
+            nc.scalar.copy(out=h_int(half, j).rearrange("p (r t) -> p r t", t=4), in_=hsum[half, j][:].rearrange("p (t r) -> p r t", t=4))
 
         def h_quant(half, j):
             toks = slice(128 * j, 128 * j + 128)
@@ -463,11 +468,13 @@ def tile_patch_embed_qkv_d4_kernel(tc, x_bytes, x_scale, w_bytes, w_scale, gain,
         quant_and_multiply(shared)
         for u in last_units:
             product_1(u, False, u == shared, [2])
+        product_1(last_units.pop(0), False, False, [3])
         h_gain(0, 2)
         free_bank((0, 2))
         h_add(0, 1, 1, range(2, 4))
         free_bank((0, 1))
         h_weave(0, 1)
+        h_gain(1, 2)
         h_add(1, 0, 1, range(0, 2))
         h_add(1, 0, 1, range(2, 4))
         h_quant(0, 0)
@@ -476,13 +483,14 @@ def tile_patch_embed_qkv_d4_kernel(tc, x_bytes, x_scale, w_bytes, w_scale, gain,
             product_2(n, range(0, 1))
         h_add(1, 1, 1, range(0, 2))
         h_quant(1, 0)
+        h_quant(0, 1)
         h_pos(0, 2)
         h_add(1, 1, 1, range(2, 4))
         h_weave(1, 1)
-        h_add(1, 2)
+        h_gain(0, 3)
+        h_weave_sum(0, 2)
         for n in (2, 1, 0):
             free_bank((1, n))
-        h_weave(1, 2)
         for n in range(3):
             product_2(n, range(1, 2))
         for n in range(3, COLUMN_BLOCKS):
@@ -493,15 +501,19 @@ def tile_patch_embed_qkv_d4_kernel(tc, x_bytes, x_scale, w_bytes, w_scale, gain,
         ready = COLUMN_BLOCKS
         for n in range(TOKEN_TILES * COLUMN_BLOCKS):
             finish(n)
-            if n == 0:
-                for h in range(2):
-                    h_gain(h, 3)
-            if n == Q2:
-                for j in (1, 2):
-                    h_quant(1, j)
-                    h_quant(0, j)
+            if n == Q1:
+                h_quant(1, 1)
+                h_pos(1, 2)
                 h_pos(0, 3)
+                h_gain(1, 3)
+                h_weave_sum(1, 2)
+                h_weave_sum(0, 3)
+                ready = 2 * COLUMN_BLOCKS
+            if n == Q2:
+                h_quant(0, 2)
+                h_quant(1, 2)
                 h_pos(1, 3)
+                h_weave_sum(1, 3)
                 ready = 3 * COLUMN_BLOCKS
             if n == COLUMN_BLOCKS:
                 free_bank((0, 3))

@@ -20,26 +20,19 @@ PASS = 512
 TOK, K, D, N = 512, 3072, 1024, 3072
 IMAGE = 256
 PASSES = K // PASS
-UNITS = 2 * PASSES
 TOKEN_TILES = TOK // P
 COLUMN_BLOCKS = N // 512
+OUT_TILES = TOKEN_TILES * COLUMN_BLOCKS
 FLOPS = 2 * TOK * K * D + 2 * TOK * D * N
 
-EARLY = 4
-SCALAR_BLOCKS = 12
-LAID = (0, 0, 2, 2, 2, 2, 2)
 SPLIT_PASSES = 2
-EXTRA = (3,)
-HALF_1 = (8, 6, 7, 9, 10, 11)
-GPSIMD_TILES = ()
-SCALAR_STORES = (15, 19, 22)
-LATE_STORE = 7
-Q1 = 1
-Q2 = 8
-PARTS = 4
-SUM_PLACE = {(0, 2): "hint10", (1, 2): "hint11", (1, 3): "hint12"}
-Q3 = 14
-STORES = ((512, 512, 1024, 1024), (1024, 1024, 1024), (1024, 1024, 1024), (1024, 1024, 512, 512))
+SCALAR_UNITS = (8, 6, 7)
+LAID_UNITS = (2, 3, 4, 5, 11)
+EARLY_TILES = 3
+AHEAD = 5
+QUANTISE_AFTER = (1, 8, 14)
+STORES = ((512,) * 6, (1024,) * 3, (1024,) * 3, (1024,) * 3)
+SCALAR_STORES = (15, 19, 23)
 
 
 def tile_patch_embed_qkv_d4_kernel(tc, x_bytes, x_scale, w_bytes, w_scale, gain, pos, v_words, v_scales, bias, out):
@@ -54,24 +47,6 @@ def tile_patch_embed_qkv_d4_kernel(tc, x_bytes, x_scale, w_bytes, w_scale, gain,
         def bank(b, dtype=F32):
             return psum.tile([P, 512 if dtype == F32 else 1024], dtype, name="bank%d" % b)
 
-        ring = list(range(8))
-
-        def next_bank(dtype=F32, ring=ring):
-            b = ring.pop(0)
-            ring.append(b)
-            return bank(b, dtype)
-
-        x_ring, w_ring = [4, 5, 6, 7], [6, 7]
-
-        held = {}
-
-        def hold_bank(key):
-            held[key] = ring.pop(0)
-            return bank(held[key])
-
-        def free_bank(key):
-            ring.insert(0, held.pop(key))
-
         ident = keep.tile([P, P], F32, name="ident")
         make_identity(nc, ident[:])
         ident_b = keep.tile([P, P], BF16, name="ident_b")
@@ -83,12 +58,13 @@ def tile_patch_embed_qkv_d4_kernel(tc, x_bytes, x_scale, w_bytes, w_scale, gain,
         nc.scalar.dma_start(out=gain_b[:].rearrange("p (h t) -> p h t", h=2), in_=gain.rearrange("(h p t) -> p h t", h=2, t=4))
 
         x_rows = x_bytes.rearrange("(a p i) k -> a p i k", a=2, i=2)
-        xb = {}
-        wb = {}
+        xb, wb = {}, {}
 
         def load_x(tiles, pair):
             t = keep.tile([P, 1024 * len(tiles)], U8, name="xb%d%d" % (tiles[0], pair))
-            nc.sync.dma_start(out=t[:].rearrange("p (j k) -> p j k", k=1024), in_=x_rows[tiles[0] // 2, :, tiles[0] % 2:tiles[-1] % 2 + 1, 1024 * pair:1024 * pair + 1024])
+            nc.sync.dma_start(
+                out=t[:].rearrange("p (j k) -> p j k", k=1024),
+                in_=x_rows[tiles[0] // 2, :, tiles[0] % 2:tiles[-1] % 2 + 1, 1024 * pair:1024 * pair + 1024])
             for n, j in enumerate(tiles):
                 xb[j, pair] = t[:, 1024 * n:1024 * n + 1024]
 
@@ -143,7 +119,7 @@ def tile_patch_embed_qkv_d4_kernel(tc, x_bytes, x_scale, w_bytes, w_scale, gain,
 
         def x_widen(g, tiles):
             if g not in xw:
-                xw[g] = stage.tile([P, 512 * EARLY], BF16, name="xw")
+                xw[g] = stage.tile([P, 512 * TOKEN_TILES], BF16, name="xw")
             for j in tiles:
                 for c in range(4):
                     src = 512 * (g % 2) + 128 * c
@@ -153,26 +129,23 @@ def tile_patch_embed_qkv_d4_kernel(tc, x_bytes, x_scale, w_bytes, w_scale, gain,
                         in0=xb[j, g // 2][:, src:src + 128].bitcast(FP8).rearrange("p (q u e) -> p q u e", u=2, e=2),
                         scalar1=xs[:, col:col + 1], scalar2=None, op0=MULT)
 
-        def x_turn(g, tiles):
+        def x_turn(g, image, b):
             words = xw[g][:].bitcast(F32)
-            xbank[g, tiles[0]] = next_bank(F32, x_ring)
-            for n, j in enumerate(tiles):
-                for u in range(2):
-                    first = 256 * j + 128 * u
-                    at = 128 * (2 * n + u)
-                    nc.tensor.transpose(xbank[g, tiles[0]][:, at:at + 128], words[:, first:first + 128], ident[:])
+            xbank[g, image] = bank(b)
+            for n in range(4):
+                first = 512 * image + 128 * n
+                nc.tensor.transpose(xbank[g, image][:, 128 * n:128 * n + 128], words[:, first:first + 128], ident[:])
 
-        def x_out(g, tiles):
+        def x_out(g, image):
             if g not in xint:
-                xint[g] = stage.tile([P, 512 * EARLY], BF16, name="xint", align_bytes=64)
-            n = len(tiles)
+                xint[g] = stage.tile([P, 512 * TOKEN_TILES], BF16, name="xint", align_bytes=64)
             nc.scalar.copy(
-                out=xint[g][:, 512 * tiles[0]:512 * (tiles[0] + n)].bitcast(F32).rearrange("p (i r u) -> p i r u", i=n, u=2),
-                in_=xbank[g, tiles[0]][:, 0:256 * n].rearrange("p (i u r) -> p i r u", i=n, u=2))
+                out=xint[g][:, 1024 * image:1024 * image + 1024].bitcast(F32).rearrange("p (i r u) -> p i r u", i=2, u=2),
+                in_=xbank[g, image][:].rearrange("p (i u r) -> p i r u", i=2, u=2))
 
         def x_quant(g):
-            xq[g] = keep.tile([P, 128 * EARLY], U32, name="xq%d" % g, align_bytes=64)
-            xqs[g] = keep.tile([P, 128 * EARLY], U8, name="xqs%d" % g, align_bytes=64)
+            xq[g] = keep.tile([P, TOK], U32, name="xq%d" % g, align_bytes=64)
+            xqs[g] = keep.tile([P, TOK], U8, name="xqs%d" % g, align_bytes=64)
             nc.vector.quantize_mx(out=xq[g][:].bitcast(FP8X4), scales=xqs[g][:], in_=xint[g][:])
 
         ww, wint, wq, wqs, wbank = {}, {}, {}, {}, {}
@@ -189,9 +162,9 @@ def tile_patch_embed_qkv_d4_kernel(tc, x_bytes, x_scale, w_bytes, w_scale, gain,
             for j in range(parts):
                 nc.scalar.copy(out=tile[:, n * j:n * j + n], in_=wb[u][:, n * j:n * j + n].bitcast(FP8))
 
-        def w_int(u, on_scalar):
+        def w_int(u):
             if u not in wint:
-                wint[u] = stage.tile([P, 2048], BF16, name="wint_s" if on_scalar else "wint_v", align_bytes=64)
+                wint[u] = stage.tile([P, 2048], BF16, name="wint_s" if u in SCALAR_UNITS else "wint_v", align_bytes=64)
             return wint[u]
 
         def w_scale_col(u, b):
@@ -199,27 +172,28 @@ def tile_patch_embed_qkv_d4_kernel(tc, x_bytes, x_scale, w_bytes, w_scale, gain,
             col = 32 * g + 4 * half + b
             return wsc[:, col:col + 1]
 
-        def w_weave(u, b, on_scalar):
-            walk = "p b m t j" if on_scalar else "p b m j t"
-            src = ww[u].rearrange("p j (b m t) -> " + walk, b=4, t=4)[:, b]
-            dst = w_int(u, on_scalar)[:].rearrange("p (t b m j) -> " + walk, t=4, b=4, j=4)[:, b]
-            if on_scalar:
-                nc.scalar.activation(out=dst, in_=src, func=COPY, scale=w_scale_col(u, b))
-            else:
-                nc.vector.tensor_scalar(out=dst, in0=src, scalar1=w_scale_col(u, b), scalar2=None, op0=MULT)
+        def w_weave(u, blocks):
+            walk = "p b m t j" if u in SCALAR_UNITS else "p b m j t"
+            for b in blocks:
+                src = ww[u].rearrange("p j (b m t) -> " + walk, b=4, t=4)[:, b]
+                dst = w_int(u)[:].rearrange("p (t b m j) -> " + walk, t=4, b=4, j=4)[:, b]
+                if u in SCALAR_UNITS:
+                    nc.scalar.activation(out=dst, in_=src, func=COPY, scale=w_scale_col(u, b))
+                else:
+                    nc.vector.tensor_scalar(out=dst, in0=src, scalar1=w_scale_col(u, b), scalar2=None, op0=MULT)
 
-        def w_lay(u, blocks):
-            tile = next_bank(BF16, w_ring)
-            for n, b in enumerate(blocks):
-                wbank[u, b] = tile[:, 512 * n:512 * n + 512]
+        def w_lay(u):
+            tile = bank(6 + LAID_UNITS.index(u) % 2, BF16)
+            for b in (2, 3):
+                wbank[u, b] = tile[:, 512 * (b - 2):512 * (b - 1)]
                 nc.tensor.matmul(
                     wbank[u, b].rearrange("p (t m j) -> p m t j", t=4, j=4), lhsT=ident_b[:],
                     rhs=ww[u][:, :, 128 * b:128 * b + 128].rearrange("p j (m t) -> p m t j", t=4), start=True, stop=True)
 
-        def w_exit(u, blocks):
-            for b in blocks:
+        def w_exit(u):
+            for b in (2, 3):
                 nc.vector.tensor_scalar(
-                    out=w_int(u, False)[:].rearrange("p (t b c) -> p b t c", t=4, b=4)[:, b],
+                    out=w_int(u)[:].rearrange("p (t b c) -> p b t c", t=4, b=4)[:, b],
                     in0=wbank[u, b].rearrange("p (t c) -> p t c", t=4), scalar1=w_scale_col(u, b), scalar2=None, op0=MULT)
 
         def w_quant(u, parts=1):
@@ -230,37 +204,34 @@ def tile_patch_embed_qkv_d4_kernel(tc, x_bytes, x_scale, w_bytes, w_scale, gain,
                 nc.vector.quantize_mx(
                     out=wq[u][:, n * j:n * j + n].bitcast(FP8X4), scales=wqs[u][:, n * j:n * j + n], in_=wint[u][:, 4 * n * j:4 * n * (j + 1)])
 
-        e, ebank = {}, {}
+        ebank, passes_added = {}, {}
 
-        def mm1(dst, u, t, rhs, rhs_scale, start, stop):
-            cols = slice(128 * t, 128 * t + 128)
-            nc.tensor.matmul_mx(out=dst, lhsT=wq[u][:, cols].bitcast(FP8X4), lhsT_scale=wqs[u][:, cols],
-                                rhs=rhs.bitcast(FP8X4), rhs_scale=rhs_scale, start=start, stop=stop)
+        def e_slice(half, j, t):
+            if j < 2:
+                return ebank[half, t // 2][:, IMAGE * (t % 2) + 128 * j:IMAGE * (t % 2) + 128 * j + 128]
+            return ebank[half, j][:, 128 * t:128 * t + 128]
 
-        def open_sums(half):
-            for n in range(4):
-                ebank[half, n] = hold_bank((half, n))
-
-        def product_1(u, first, last, images=range(2)):
+        def product_1(u, banks=range(4)):
             half, g = divmod(u, PASSES)
-            if 0 in images:
-                for t in range(4):
-                    dst = ebank[half, t // 2][:, IMAGE * (t % 2):IMAGE * (t % 2) + IMAGE]
-                    e[half, t, 0] = dst
-                    mm1(dst, u, t, xq[g][:, 0:IMAGE], xqs[g][:, 0:IMAGE], first and t % 2 == 0, last and t % 2 == 1)
-            for j in (2, 3):
-                if j in images or 1 in images:
-                    toks = slice(128 * j, 128 * j + 128)
-                    for t in range(4):
-                        dst = ebank[half, j][:, 128 * t:128 * t + 128]
-                        e[half, t, j] = dst
-                        mm1(dst, u, t, xq[g][:, toks], xqs[g][:, toks], first and t == 0, last and t == 3)
+            for n in banks:
+                if (half, n) not in ebank:
+                    ebank[half, n] = bank(4 * half + n)
+                passes_added[half, n] = passes_added.get((half, n), 0) + 1
+                slices = (2 * n, 2 * n + 1) if n < 2 else range(4)
+                toks = slice(0, IMAGE) if n < 2 else slice(128 * n, 128 * n + 128)
+                for t in slices:
+                    cols = slice(128 * t, 128 * t + 128)
+                    nc.tensor.matmul_mx(
+                        out=ebank[half, n][:, IMAGE * (t % 2):IMAGE * (t % 2) + IMAGE] if n < 2 else e_slice(half, n, t),
+                        lhsT=wq[u][:, cols].bitcast(FP8X4), lhsT_scale=wqs[u][:, cols],
+                        rhs=xq[g][:, toks].bitcast(FP8X4), rhs_scale=xqs[g][:, toks],
+                        start=passes_added[half, n] == 1 and t == slices[0], stop=passes_added[half, n] == PASSES and t == slices[-1])
 
         pos_t = keep.tile([P, 2048], BF16, name="pos_t")
         pos_bank = {}
 
-        def pos_turn(half):
-            pos_bank[half] = next_bank(F32, ring if half else x_ring)
+        def pos_turn(half, b):
+            pos_bank[half] = bank(b)
             words = pos_sb[:].bitcast(F32)
             for u in range(2):
                 for i in range(2):
@@ -276,50 +247,46 @@ def tile_patch_embed_qkv_d4_kernel(tc, x_bytes, x_scale, w_bytes, w_scale, gain,
         hq = [keep.tile([P, TOK], U32, name="hq%d" % h, align_bytes=64) for h in range(2)]
         hqs = [keep.tile([P, TOK], U8, name="hqs%d" % h, align_bytes=64) for h in range(2)]
 
-        def h_add(half, j, n=1, slices=range(4)):
-            lo, hi = 128 * j, 128 * (j + n)
-            r = lo % IMAGE
+        def h_add(half, tiles, slices):
+            lo, hi = 128 * tiles[0], 128 * tiles[-1] + 128
             for t in slices:
-                at = 1024 * half + 2 * IMAGE * (t // 2) + 2 * r + t % 2
-                src = e[half, t, 0][:, lo:hi] if j < 2 else e[half, t, j]
+                at = 1024 * half + 2 * IMAGE * (t // 2) + 2 * lo + t % 2
                 nc.vector.scalar_tensor_tensor(
-                    out=hs[half][:, TOK * t + lo:TOK * t + hi], in0=src,
+                    out=hs[half][:, TOK * t + lo:TOK * t + hi], in0=ebank[half, t // 2][:, IMAGE * (t % 2) + lo:IMAGE * (t % 2) + hi],
                     scalar=gain_f[:, 4 * half + t:4 * half + t + 1], in1=pos_t[:, at:at + 2 * (hi - lo) - 1:2], op0=MULT, op1=ADD)
-
-        def h_int(half, j):
-            hint[half, j] = keep.tile([P, 512], BF16, name="hint%d%d" % (half, j), align_bytes=64)
-            return hint[half, j][:]
-
-        def h_weave(half, j, copy=nc.scalar.copy):
-            copy(
-                out=h_int(half, j).rearrange("p (r t) -> p r t", t=4),
-                in_=hs[half][:].rearrange("p (t r) -> p r t", t=4)[:, 128 * j:128 * j + 128])
 
         def h_gain(half, j):
             h32[half, j] = keep.tile([P, 512], F32, name="h32%d%d" % (half, j))
             for t in range(4):
-                nc.scalar.activation(out=h32[half, j][:, 128 * t:128 * t + 128], in_=e[half, t, j], func=COPY, scale=gain_f[:, 4 * half + t:4 * half + t + 1])
+                nc.scalar.activation(
+                    out=h32[half, j][:, 128 * t:128 * t + 128], in_=e_slice(half, j, t), func=COPY, scale=gain_f[:, 4 * half + t:4 * half + t + 1])
 
-        def h_pos(half, j):
-            hsum[half, j] = keep.tile([P, 512], BF16, name=SUM_PLACE.get((half, j), "hsum%d%d" % (half, j)), align_bytes=64)
+        def h_pos(half, j, buffer):
+            hsum[half, j] = keep.tile([P, 512], BF16, name=buffer, align_bytes=64)
             nc.gpsimd.tensor_tensor(
                 out=hsum[half, j][:].rearrange("p (u e r) -> p u e r", u=2, e=2),
                 in0=h32[half, j][:].rearrange("p (u e r) -> p u e r", u=2, e=2),
                 in1=pos_t[:].rearrange("p (h u i r e) -> p h i u e r", h=2, u=2, i=2, e=2)[:, half, j % 2], op=ADD)
 
-        def h_weave_sum(half, j):
-            nc.scalar.copy(out=h_int(half, j).rearrange("p (r t) -> p r t", t=4), in_=hsum[half, j][:].rearrange("p (t r) -> p r t", t=4))
+        def h_weave(half, j, copy=nc.scalar.copy):
+            hint[half, j] = keep.tile([P, 512], BF16, name="hint%d%d" % (half, j), align_bytes=64)
+            if j < 2:
+                planes = hs[half][:].rearrange("p (t r) -> p r t", t=4)[:, 128 * j:128 * j + 128]
+            else:
+                planes = hsum[half, j][:].rearrange("p (t r) -> p r t", t=4)
+            copy(out=hint[half, j][:].rearrange("p (r t) -> p r t", t=4), in_=planes)
 
         def h_quant(half, j):
             toks = slice(128 * j, 128 * j + 128)
             nc.vector.quantize_mx(out=hq[half][:, toks].bitcast(FP8X4), scales=hqs[half][:, toks], in_=hint[half, j][:])
 
-        ob, ot = {}, {}
+        ob, ot, out_banks = {}, {}, []
 
         def product_2(n, halves=range(2)):
             i, c = divmod(n, COLUMN_BLOCKS)
             if n not in ob:
-                ob[n] = next_bank()
+                out_banks.append(out_banks.pop(0))
+                ob[n] = bank(out_banks[-1])
             toks = slice(128 * i, 128 * i + 128)
             for h in halves:
                 nc.tensor.matmul_mx(
@@ -328,200 +295,150 @@ def tile_patch_embed_qkv_d4_kernel(tc, x_bytes, x_scale, w_bytes, w_scale, gain,
                     rhs=vw[h][:, 1024 * c:1024 * c + 1024].bitcast(FP4X4), rhs_scale=vs[:, N * h + 512 * c:N * h + 512 * c + 512],
                     start=(h == 0), stop=(h == 1))
 
-        waiting = []
-
-        def store(i, first, width, queue):
-            rows = out.rearrange("(a p i) n -> a i p n", a=2, i=2)[i // 2, i % 2]
-            queue.dma_start(out=rows[:, first:first + width], in_=ot[i, first][:, 0:width])
-
         def finish(n):
             i, c = divmod(n, COLUMN_BLOCKS)
             first = 0
             for width in STORES[i]:
                 if first <= 512 * c < first + width:
                     if 512 * c == first:
-                        ot[i, first] = wide.tile([P, width], F32, name="wide_pass" if width > 1024 or len(ot) % 2 == 0 else "wide_unit")
-                    o = ot[i, first][:, 512 * c - first:512 * c - first + 512]
-                    cols = slice(512 * c, 512 * c + 512)
-                    if n in GPSIMD_TILES:
-                        nc.scalar.copy(out=o, in_=ob[n][:])
-                        nc.gpsimd.tensor_tensor(out=o, in0=o, in1=bias_sb[:, cols], op=ADD)
-                    else:
-                        nc.vector.tensor_tensor(out=o, in0=ob[n][:], in1=bias_sb[:, cols], op=ADD)
+                        ot[i, first] = wide.tile([P, width], F32, name="wide_pass" if len(ot) % 2 == 0 else "wide_unit")
+                    nc.vector.tensor_tensor(
+                        out=ot[i, first][:, 512 * c - first:512 * c - first + 512], in0=ob[n][:], in1=bias_sb[:, 512 * c:512 * c + 512], op=ADD)
                     if 512 * c + 512 == first + width:
-                        if n in GPSIMD_TILES:
-                            waiting.append((i, first, width))
-                        else:
-                            store(i, first, width, nc.scalar if n in SCALAR_STORES else nc.sync)
+                        rows = out.rearrange("(a p i) n -> a i p n", a=2, i=2)[i // 2, i % 2]
+                        queue = nc.scalar if n in SCALAR_STORES else nc.sync
+                        queue.dma_start(out=rows[:, first:first + width], in_=ot[i, first][:])
                 first = first + width
 
-        blocks = [(u, b) for u in HALF_1 for b in range(4)]
-        scalar_blocks = blocks[:SCALAR_BLOCKS]
-        shared = scalar_blocks[-1][0]
-        scalar_units = list(HALF_1[:list(HALF_1).index(shared)])
-        vector_units = list(range(PASSES)) + list(reversed(HALF_1[list(HALF_1).index(shared):]))
-        laid = {u: list(range(4 - n, 4)) for u, n in zip(vector_units, LAID)}
-        theirs = list(scalar_blocks)
-
-        def lay(u):
-            bs = laid.get(u, [])
-            for n in range(0, len(bs), 2):
-                w_lay(u, bs[n:n + 2])
-
-        def vector_weave(u):
-            for b in range(4):
-                if (u, b) not in theirs and b not in laid.get(u, []):
-                    w_weave(u, b, False)
-
-        def scalar_weave(n):
-            for j in range(min(n, len(scalar_blocks))):
-                w_weave(*scalar_blocks.pop(0), True)
-
-        open_sums(0)
         nc.scalar.activation(out=gain_f[:], in_=gain_b[:], func=COPY)
         for j in range(2):
             for g in range(2):
                 x_widen(g, [j])
-        x_turn(0, [0, 1])
+        x_turn(0, 0, 4)
         w_widen(0, 2)
         for j in range(2, 4):
             for g in range(2):
                 x_widen(g, [j])
-        x_turn(0, [2, 3])
-        x_turn(1, [0, 1])
-        x_out(0, [0, 1])
+        x_turn(0, 1, 5)
+        x_turn(1, 0, 6)
+        x_out(0, 0)
         w_widen(1)
-        x_out(0, [2, 3])
-        x_turn(1, [2, 3])
-        x_ring.remove(6)
-        x_ring.remove(7)
-        vector_weave(0)
-        for s in range(PASSES):
-            u = vector_units[s + 1]
-            if s + 1 < PASSES:
-                x_out(s + 1, [0, 1])
-                x_out(s + 1, [2, 3])
-            if s + 2 < PASSES:
-                w_widen(s + 2)
-                x_widen(s + 2, range(4))
-            if s in EXTRA:
-                scalar_weave(1)
+        x_out(0, 1)
+        x_turn(1, 1, 7)
+        w_weave(0, range(4))
+
+        for s in range(PASSES - 2):
+            x_out(s + 1, 0)
+            x_out(s + 1, 1)
+            w_widen(s + 2)
+            x_widen(s + 2, range(4))
+            if s + 2 == PASSES - 1:
+                w_weave(8, [0])
             if s > 0:
-                product_1(s - 1, s == 1, False, [0])
-            if s + 2 < PASSES:
-                vector_weave(u)
-                x_turn(s + 2, [0, 1])
-                x_turn(s + 2, [2, 3])
-            if s + 2 == PASSES:
-                pos_turn(0)
-                w_widen(PASSES)
-                pos_out(0)
-                scalar_weave(4 - len(EXTRA))
-                w_widen(PASSES + 1)
-                scalar_weave(len(scalar_blocks))
+                product_1(s - 1, [0, 1])
+            w_weave(s + 1, range(2 if s + 1 in LAID_UNITS else 4))
+            x_turn(s + 2, 0, 4)
+            x_turn(s + 2, 1, 5)
             if s > 0:
-                product_1(s - 1, s == 1, False, [1])
+                product_1(s - 1, [2, 3])
             x_quant(s)
-            if s + 2 < PASSES:
-                w_exit(u, laid.get(u, []))
-                w_quant(s)
-            else:
-                w_quant(s)
-                vector_weave(u)
-                w_exit(u, laid.get(u, []))
-            lay(vector_units[s + 2])
-        product_1(PASSES - 1, False, True)
+            if s + 1 in LAID_UNITS:
+                w_exit(s + 1)
+            w_quant(s)
+            w_lay(s + 2)
 
-        open_sums(1)
+        x_out(5, 0)
+        x_out(5, 1)
+        product_1(3, [0, 1])
+        pos_turn(0, 4)
+        w_widen(6)
+        pos_out(0)
+        w_weave(8, range(1, 4))
+        w_widen(7)
+        w_weave(6, range(4))
+        w_weave(7, range(4))
+        product_1(3, [2, 3])
+        x_quant(4)
+        w_quant(4)
+        w_weave(5, range(2))
+        w_exit(5)
+        w_lay(11)
+        product_1(4)
+        x_quant(5)
+        w_quant(5)
+        w_weave(11, range(2))
+        w_exit(11)
+        product_1(5)
 
-        done, last_units = [], []
-
-        def quant_and_multiply(u):
-            w_quant(u, PARTS if u == shared else 1)
-            if len(done) < 3:
-                product_1(u, not done, False)
-            else:
-                product_1(u, False, u == shared, [0])
-                last_units.append(u)
-            done.append(u)
-
-        rest = vector_units[PASSES:]
-        for n, u in enumerate(rest[1:]):
-            if n == 0:
-                w_weave(u, 0, False)
-                quant_and_multiply(rest[0])
-                theirs.append((u, 0))
-            vector_weave(u)
-            if scalar_units:
-                quant_and_multiply(scalar_units.pop(0))
-            if n == 0:
-                h_add(0, 0, 2, range(0, 2))
-                free_bank((0, 0))
-                pos_turn(1)
-            if u != shared:
-                quant_and_multiply(u)
-        for u in scalar_units:
-            quant_and_multiply(u)
-        h_add(0, 0, 1, range(2, 4))
+        w_weave(10, [0])
+        w_quant(11)
+        product_1(11)
+        w_weave(10, range(1, 4))
+        w_quant(8)
+        product_1(8)
+        h_add(0, [0, 1], range(2))
+        pos_turn(1, 0)
+        w_quant(10)
+        product_1(10)
+        w_weave(9, range(4))
+        for u in (6, 9):
+            w_quant(u)
+            product_1(u, [0, 1])
+        h_add(0, [0], range(2, 4))
         pos_out(1)
         h_weave(0, 0)
-        quant_and_multiply(shared)
-        for u in last_units:
-            product_1(u, False, u == shared, [2])
-        product_1(last_units.pop(0), False, False, [3])
+        w_quant(7, 4)
+        product_1(7, [0, 1])
+        for u in (6, 9, 7):
+            product_1(u, [2])
+        product_1(6, [3])
+
         h_gain(0, 2)
-        free_bank((0, 2))
-        h_add(0, 1, 1, range(2, 4))
-        free_bank((0, 1))
+        h_add(0, [1], range(2, 4))
         h_weave(0, 1)
         h_gain(1, 2)
-        h_add(1, 0, 1, range(0, 2))
-        h_add(1, 0, 1, range(2, 4))
+        h_add(1, [0], range(4))
         h_quant(0, 0)
         h_weave(1, 0, copy=nc.vector.tensor_copy)
-        for n in range(3):
-            product_2(n, range(0, 1))
-        h_add(1, 1, 1, range(0, 2))
+        out_banks.extend([1, 2, 0])
+        for n in range(EARLY_TILES):
+            product_2(n, [0])
+        h_add(1, [1], range(2))
         h_quant(1, 0)
         h_quant(0, 1)
-        h_pos(0, 2)
-        h_add(1, 1, 1, range(2, 4))
+        h_pos(0, 2, "hint10")
+        h_add(1, [1], range(2, 4))
         h_weave(1, 1)
         h_gain(0, 3)
-        h_weave_sum(0, 2)
-        for n in (2, 1, 0):
-            free_bank((1, n))
-        for n in range(3):
-            product_2(n, range(1, 2))
-        for n in range(3, COLUMN_BLOCKS):
-            product_2(n)
-        for u in last_units:
-            product_1(u, False, u == shared, [3])
-        issued = COLUMN_BLOCKS
-        ready = COLUMN_BLOCKS
-        for n in range(TOKEN_TILES * COLUMN_BLOCKS):
+        h_weave(0, 2)
+        out_banks[0:0] = [4, 5, 6]
+        for n in range(COLUMN_BLOCKS):
+            product_2(n, [1] if n < EARLY_TILES else range(2))
+        for u in (9, 7):
+            product_1(u, [3])
+
+        issued = ready = COLUMN_BLOCKS
+        for n in range(OUT_TILES):
             finish(n)
-            if n == Q1:
+            if n == QUANTISE_AFTER[0]:
                 h_quant(1, 1)
-                h_pos(1, 2)
-                h_pos(0, 3)
+                h_pos(1, 2, "hint11")
+                h_pos(0, 3, "hsum03")
                 h_gain(1, 3)
-                h_weave_sum(1, 2)
-                h_weave_sum(0, 3)
-                ready = 2 * COLUMN_BLOCKS
-            if n == Q2:
+                h_weave(1, 2)
+                h_weave(0, 3)
+            if n == QUANTISE_AFTER[1]:
                 h_quant(0, 2)
                 h_quant(1, 2)
-                h_pos(1, 3)
-                h_weave_sum(1, 3)
-                ready = 3 * COLUMN_BLOCKS
-            if n == COLUMN_BLOCKS:
-                free_bank((0, 3))
-                free_bank((1, 3))
-            if n == Q3:
+                h_pos(1, 3, "hint12")
+                h_weave(1, 3)
+            if n == QUANTISE_AFTER[2]:
                 h_quant(0, 3)
                 h_quant(1, 3)
-                ready = 4 * COLUMN_BLOCKS
-            for m in range(issued, min(n + 5, ready)):
+            if n in QUANTISE_AFTER:
+                ready = ready + COLUMN_BLOCKS
+            if n == COLUMN_BLOCKS:
+                out_banks[0:0] = [7, 3]
+            for m in range(issued, min(n + AHEAD, ready)):
                 product_2(m)
-            issued = max(issued, min(n + 5, ready))
+            issued = max(issued, min(n + AHEAD, ready))

from contextlib import ExitStack

import concourse.mybir as mybir
from concourse.masks import make_identity

F32 = mybir.dt.float32
BF16 = mybir.dt.bfloat16
I32 = mybir.dt.int32
U32 = mybir.dt.uint32
U8 = mybir.dt.uint8
FP8 = mybir.dt.float8_e4m3fn
FP8X4 = mybir.dt.float8_e4m3fn_x4
FP4X4 = mybir.dt.float4_e2m1fn_x4
MULT = mybir.AluOpType.mult
ADD = mybir.AluOpType.add
COPY = mybir.ActivationFunctionType.Copy

P = 128
PASS = 512
TOK, K, D, N = 512, 3072, 1024, 3072
IMAGE = 256
PASSES = K // PASS
TOKEN_TILES = TOK // P
COLUMN_BLOCKS = N // 512
OUT_TILES = TOKEN_TILES * COLUMN_BLOCKS
FLOPS = 2 * TOK * K * D + 2 * TOK * D * N

SPLIT_PASSES = 2
SCALAR_UNITS = (8, 6, 7)
LAID_UNITS = (2, 3, 4, 5, 11)
EARLY_TILES = 3
AHEAD = 5
QUANTISE_AFTER = (1, 8, 14)
STORES = ((512,) * 6, (1024,) * 3, (1024,) * 3, (1024,) * 3)
SCALAR_STORES = (15, 19, 23)


def tile_patch_embed_qkv_d4_kernel(tc, x_bytes, x_scale, w_bytes, w_scale, gain, pos, v_words, v_scales, bias, out):
    nc = tc.nc
    with ExitStack() as ctx:
        keep = ctx.enter_context(tc.tile_pool(name="keep", bufs=1))
        stage = ctx.enter_context(tc.tile_pool(name="stage", bufs=3))
        wide = ctx.enter_context(tc.tile_pool(name="wide", bufs=4))
        psum = ctx.enter_context(tc.psum_pool(name="psum", bufs=1))
        ctx.enter_context(tc.manual_schedule())

        def bank(b, dtype=F32):
            return psum.tile([P, 512 if dtype == F32 else 1024], dtype, name="bank%d" % b)

        ident = keep.tile([P, P], F32, name="ident")
        make_identity(nc, ident[:])
        ident_b = keep.tile([P, P], BF16, name="ident_b")
        make_identity(nc, ident_b[:])

        xs = keep.tile([P, TOKEN_TILES * 24], F32, name="xs")
        nc.scalar.dma_start(out=xs[:].rearrange("p (a c) -> p a c", a=2), in_=x_scale.rearrange("(a p i) c -> p a (i c)", a=2, i=2))
        gain_b = keep.tile([P, 8], BF16, name="gain_b")
        nc.scalar.dma_start(out=gain_b[:].rearrange("p (h t) -> p h t", h=2), in_=gain.rearrange("(h p t) -> p h t", h=2, t=4))

        x_rows = x_bytes.rearrange("(a p i) k -> a p i k", a=2, i=2)
        xb, wb = {}, {}

        def load_x(tiles, pair):
            t = keep.tile([P, 1024 * len(tiles)], U8, name="xb%d%d" % (tiles[0], pair))
            nc.sync.dma_start(
                out=t[:].rearrange("p (j k) -> p j k", k=1024),
                in_=x_rows[tiles[0] // 2, :, tiles[0] % 2:tiles[-1] % 2 + 1, 1024 * pair:1024 * pair + 1024])
            for n, j in enumerate(tiles):
                xb[j, pair] = t[:, 1024 * n:1024 * n + 1024]

        def load_w(u, rows_t=slice(0, 4)):
            half, g = divmod(u, PASSES)
            rows = w_bytes[PASS * g:PASS * g + PASS, :]
            if g < SPLIT_PASSES:
                if u not in wb:
                    wb[u] = keep.tile([P, 2048], U8, name="wb%d" % u)
                nc.sync.dma_start(
                    out=wb[u][:].rearrange("p (t n) -> p t n", t=4)[:, rows_t],
                    in_=rows[:, 512 * half:512 * half + 512].rearrange("(p t) n -> p t n", t=4)[:, rows_t])
            else:
                wb[u] = keep.tile([P, 4096], U8, name="wb%d" % u)
                nc.sync.dma_start(out=wb[u][:], in_=rows.rearrange("(p t) n -> p (t n)", t=4))

        load_x([0], 0)
        load_w(0, slice(0, 2))
        load_x([1], 0)
        load_w(0, slice(2, 4))
        load_x([2], 0)
        load_x([3], 0)
        load_w(1)
        wsc = keep.tile([P, 168], F32, name="wsc")
        for q in range(4):
            nc.sync.dma_start(out=wsc[32 * q:32 * q + 32, :], in_=w_scale.rearrange("c d -> (c d)")[8 * q:8 * q + 168].partition_broadcast(32))
        load_x([0, 1], 1)
        load_x([2, 3], 1)
        load_w(2)
        load_w(3)
        load_x([0, 1], 2)
        load_x([2, 3], 2)
        for u in (4, 5, 6, 7):
            load_w(u)
        pos_sb = keep.tile([P, 2 * D], BF16, name="pos_sb")
        nc.sync.dma_start(out=pos_sb[:], in_=pos.rearrange("(p i) j -> p (i j)", i=2))
        vw = [keep.tile([P, 2 * N], U8, name="vw%d" % h, align_bytes=64) for h in range(2)]
        for h in range(2):
            nc.sync.dma_start(out=vw[h][:].bitcast(I32), in_=v_words[h].bitcast(I32))
        vs = keep.tile([P, 2 * N], U8, name="vs", align_bytes=64)
        nc.vector.memset(vs[:].bitcast(I32), 0)
        for q in range(4):
            nc.sync.dma_start(
                out=vs[32 * q:32 * q + 4, :].rearrange("p (h n) -> p h n", h=2).bitcast(I32),
                in_=v_scales[:, 4 * q:4 * q + 4, :].rearrange("h r n -> r h n").bitcast(I32))
        bias_sb = keep.tile([P, N], BF16, name="bias_sb")
        nc.sync.dma_start(out=bias_sb[:], in_=bias.partition_broadcast(P))

        gain_f = keep.tile([P, 8], F32, name="gain_f")

        xw, xint, xq, xqs, xbank = {}, {}, {}, {}, {}

        def x_widen(g, tiles):
            if g not in xw:
                xw[g] = stage.tile([P, 512 * TOKEN_TILES], BF16, name="xw")
            for j in tiles:
                for c in range(4):
                    src = 512 * (g % 2) + 128 * c
                    col = 24 * j + 4 * g + c
                    nc.vector.tensor_scalar(
                        out=xw[g][:, 512 * j:512 * j + 512].rearrange("p (u c q e) -> p c q u e", u=2, c=4, e=2)[:, c],
                        in0=xb[j, g // 2][:, src:src + 128].bitcast(FP8).rearrange("p (q u e) -> p q u e", u=2, e=2),
                        scalar1=xs[:, col:col + 1], scalar2=None, op0=MULT)

        def x_turn(g, image, b):
            words = xw[g][:].bitcast(F32)
            xbank[g, image] = bank(b)
            for n in range(4):
                first = 512 * image + 128 * n
                nc.tensor.transpose(xbank[g, image][:, 128 * n:128 * n + 128], words[:, first:first + 128], ident[:])

        def x_out(g, image):
            if g not in xint:
                xint[g] = stage.tile([P, 512 * TOKEN_TILES], BF16, name="xint", align_bytes=64)
            nc.scalar.copy(
                out=xint[g][:, 1024 * image:1024 * image + 1024].bitcast(F32).rearrange("p (i r u) -> p i r u", i=2, u=2),
                in_=xbank[g, image][:].rearrange("p (i u r) -> p i r u", i=2, u=2))

        def x_quant(g):
            xq[g] = keep.tile([P, TOK], U32, name="xq%d" % g, align_bytes=64)
            xqs[g] = keep.tile([P, TOK], U8, name="xqs%d" % g, align_bytes=64)
            nc.vector.quantize_mx(out=xq[g][:].bitcast(FP8X4), scales=xqs[g][:], in_=xint[g][:])

        ww, wint, wq, wqs, wbank = {}, {}, {}, {}, {}

        def w_widen(u, parts=1):
            if u % PASSES < SPLIT_PASSES:
                tile = wide.tile([P, 2048], BF16, name="wide_unit")
                ww[u] = tile[:].rearrange("p (t n) -> p t n", t=4)
            else:
                tile = wide.tile([P, 4096], BF16, name="wide_pass")
                both = tile[:].rearrange("p (t n) -> p t n", t=4)
                ww[u], ww[u + PASSES] = both[:, :, 0:512], both[:, :, 512:1024]
            n = tile.shape[1] // parts
            for j in range(parts):
                nc.scalar.copy(out=tile[:, n * j:n * j + n], in_=wb[u][:, n * j:n * j + n].bitcast(FP8))

        def w_int(u):
            if u not in wint:
                wint[u] = stage.tile([P, 2048], BF16, name="wint_s" if u in SCALAR_UNITS else "wint_v", align_bytes=64)
            return wint[u]

        def w_scale_col(u, b):
            half, g = divmod(u, PASSES)
            col = 32 * g + 4 * half + b
            return wsc[:, col:col + 1]

        def w_weave(u, blocks):
            walk = "p b m t j" if u in SCALAR_UNITS else "p b m j t"
            for b in blocks:
                src = ww[u].rearrange("p j (b m t) -> " + walk, b=4, t=4)[:, b]
                dst = w_int(u)[:].rearrange("p (t b m j) -> " + walk, t=4, b=4, j=4)[:, b]
                if u in SCALAR_UNITS:
                    nc.scalar.activation(out=dst, in_=src, func=COPY, scale=w_scale_col(u, b))
                else:
                    nc.vector.tensor_scalar(out=dst, in0=src, scalar1=w_scale_col(u, b), scalar2=None, op0=MULT)

        def w_lay(u):
            tile = bank(6 + LAID_UNITS.index(u) % 2, BF16)
            for b in (2, 3):
                wbank[u, b] = tile[:, 512 * (b - 2):512 * (b - 1)]
                nc.tensor.matmul(
                    wbank[u, b].rearrange("p (t m j) -> p m t j", t=4, j=4), lhsT=ident_b[:],
                    rhs=ww[u][:, :, 128 * b:128 * b + 128].rearrange("p j (m t) -> p m t j", t=4), start=True, stop=True)

        def w_exit(u):
            for b in (2, 3):
                nc.vector.tensor_scalar(
                    out=w_int(u)[:].rearrange("p (t b c) -> p b t c", t=4, b=4)[:, b],
                    in0=wbank[u, b].rearrange("p (t c) -> p t c", t=4), scalar1=w_scale_col(u, b), scalar2=None, op0=MULT)

        def w_quant(u, parts=1):
            wq[u] = stage.tile([P, 512], U32, name="wq", align_bytes=64)
            wqs[u] = stage.tile([P, 512], U8, name="wqs", align_bytes=64)
            n = 512 // parts
            for j in range(parts):
                nc.vector.quantize_mx(
                    out=wq[u][:, n * j:n * j + n].bitcast(FP8X4), scales=wqs[u][:, n * j:n * j + n], in_=wint[u][:, 4 * n * j:4 * n * (j + 1)])

        ebank, passes_added = {}, {}

        def e_slice(half, j, t):
            if j < 2:
                return ebank[half, t // 2][:, IMAGE * (t % 2) + 128 * j:IMAGE * (t % 2) + 128 * j + 128]
            return ebank[half, j][:, 128 * t:128 * t + 128]

        def product_1(u, banks=range(4)):
            half, g = divmod(u, PASSES)
            for n in banks:
                if (half, n) not in ebank:
                    ebank[half, n] = bank(4 * half + n)
                passes_added[half, n] = passes_added.get((half, n), 0) + 1
                slices = (2 * n, 2 * n + 1) if n < 2 else range(4)
                toks = slice(0, IMAGE) if n < 2 else slice(128 * n, 128 * n + 128)
                for t in slices:
                    cols = slice(128 * t, 128 * t + 128)
                    nc.tensor.matmul_mx(
                        out=ebank[half, n][:, IMAGE * (t % 2):IMAGE * (t % 2) + IMAGE] if n < 2 else e_slice(half, n, t),
                        lhsT=wq[u][:, cols].bitcast(FP8X4), lhsT_scale=wqs[u][:, cols],
                        rhs=xq[g][:, toks].bitcast(FP8X4), rhs_scale=xqs[g][:, toks],
                        start=passes_added[half, n] == 1 and t == slices[0], stop=passes_added[half, n] == PASSES and t == slices[-1])

        pos_t = keep.tile([P, 2048], BF16, name="pos_t")
        pos_bank = {}

        def pos_turn(half, b):
            pos_bank[half] = bank(b)
            words = pos_sb[:].bitcast(F32)
            for u in range(2):
                for i in range(2):
                    first = 512 * i + 256 * half + u
                    at = IMAGE * u + 128 * i
                    nc.tensor.transpose(pos_bank[half][:, at:at + 128], words[:, first:first + 255:2], ident[:])

        def pos_out(half):
            nc.scalar.copy(out=pos_t[:, 1024 * half:1024 * half + 1024].bitcast(F32), in_=pos_bank[half][:])

        hs = [keep.tile([P, 4 * TOK], BF16, name="hs%d" % h) for h in range(2)]
        hint, h32, hsum = {}, {}, {}
        hq = [keep.tile([P, TOK], U32, name="hq%d" % h, align_bytes=64) for h in range(2)]
        hqs = [keep.tile([P, TOK], U8, name="hqs%d" % h, align_bytes=64) for h in range(2)]

        def h_add(half, tiles, slices):
            lo, hi = 128 * tiles[0], 128 * tiles[-1] + 128
            for t in slices:
                at = 1024 * half + 2 * IMAGE * (t // 2) + 2 * lo + t % 2
                nc.vector.scalar_tensor_tensor(
                    out=hs[half][:, TOK * t + lo:TOK * t + hi], in0=ebank[half, t // 2][:, IMAGE * (t % 2) + lo:IMAGE * (t % 2) + hi],
                    scalar=gain_f[:, 4 * half + t:4 * half + t + 1], in1=pos_t[:, at:at + 2 * (hi - lo) - 1:2], op0=MULT, op1=ADD)

        def h_gain(half, j):
            h32[half, j] = keep.tile([P, 512], F32, name="h32%d%d" % (half, j))
            for t in range(4):
                nc.scalar.activation(
                    out=h32[half, j][:, 128 * t:128 * t + 128], in_=e_slice(half, j, t), func=COPY, scale=gain_f[:, 4 * half + t:4 * half + t + 1])

        def h_pos(half, j, buffer):
            hsum[half, j] = keep.tile([P, 512], BF16, name=buffer, align_bytes=64)
            nc.gpsimd.tensor_tensor(
                out=hsum[half, j][:].rearrange("p (u e r) -> p u e r", u=2, e=2),
                in0=h32[half, j][:].rearrange("p (u e r) -> p u e r", u=2, e=2),
                in1=pos_t[:].rearrange("p (h u i r e) -> p h i u e r", h=2, u=2, i=2, e=2)[:, half, j % 2], op=ADD)

        def h_weave(half, j, copy=nc.scalar.copy):
            hint[half, j] = keep.tile([P, 512], BF16, name="hint%d%d" % (half, j), align_bytes=64)
            if j < 2:
                planes = hs[half][:].rearrange("p (t r) -> p r t", t=4)[:, 128 * j:128 * j + 128]
            else:
                planes = hsum[half, j][:].rearrange("p (t r) -> p r t", t=4)
            copy(out=hint[half, j][:].rearrange("p (r t) -> p r t", t=4), in_=planes)

        def h_quant(half, j):
            toks = slice(128 * j, 128 * j + 128)
            nc.vector.quantize_mx(out=hq[half][:, toks].bitcast(FP8X4), scales=hqs[half][:, toks], in_=hint[half, j][:])

        ob, ot, out_banks = {}, {}, []

        def product_2(n, halves=range(2)):
            i, c = divmod(n, COLUMN_BLOCKS)
            if n not in ob:
                out_banks.append(out_banks.pop(0))
                ob[n] = bank(out_banks[-1])
            toks = slice(128 * i, 128 * i + 128)
            for h in halves:
                nc.tensor.matmul_mx(
                    out=ob[n][:],
                    lhsT=hq[h][:, toks].bitcast(FP8X4), lhsT_scale=hqs[h][:, toks],
                    rhs=vw[h][:, 1024 * c:1024 * c + 1024].bitcast(FP4X4), rhs_scale=vs[:, N * h + 512 * c:N * h + 512 * c + 512],
                    start=(h == 0), stop=(h == 1))

        def finish(n):
            i, c = divmod(n, COLUMN_BLOCKS)
            first = 0
            for width in STORES[i]:
                if first <= 512 * c < first + width:
                    if 512 * c == first:
                        ot[i, first] = wide.tile([P, width], F32, name="wide_pass" if len(ot) % 2 == 0 else "wide_unit")
                    nc.vector.tensor_tensor(
                        out=ot[i, first][:, 512 * c - first:512 * c - first + 512], in0=ob[n][:], in1=bias_sb[:, 512 * c:512 * c + 512], op=ADD)
                    if 512 * c + 512 == first + width:
                        rows = out.rearrange("(a p i) n -> a i p n", a=2, i=2)[i // 2, i % 2]
                        queue = nc.scalar if n in SCALAR_STORES else nc.sync
                        queue.dma_start(out=rows[:, first:first + width], in_=ot[i, first][:])
                first = first + width

        nc.scalar.activation(out=gain_f[:], in_=gain_b[:], func=COPY)
        for j in range(2):
            for g in range(2):
                x_widen(g, [j])
        x_turn(0, 0, 4)
        w_widen(0, 2)
        for j in range(2, 4):
            for g in range(2):
                x_widen(g, [j])
        x_turn(0, 1, 5)
        x_turn(1, 0, 6)
        x_out(0, 0)
        w_widen(1)
        x_out(0, 1)
        x_turn(1, 1, 7)
        w_weave(0, range(4))

        for s in range(PASSES - 2):
            x_out(s + 1, 0)
            x_out(s + 1, 1)
            w_widen(s + 2)
            x_widen(s + 2, range(4))
            if s + 2 == PASSES - 1:
                w_weave(8, [0])
            if s > 0:
                product_1(s - 1, [0, 1])
            w_weave(s + 1, range(2 if s + 1 in LAID_UNITS else 4))
            x_turn(s + 2, 0, 4)
            x_turn(s + 2, 1, 5)
            if s > 0:
                product_1(s - 1, [2, 3])
            x_quant(s)
            if s + 1 in LAID_UNITS:
                w_exit(s + 1)
            w_quant(s)
            w_lay(s + 2)

        x_out(5, 0)
        x_out(5, 1)
        product_1(3, [0, 1])
        pos_turn(0, 4)
        w_widen(6)
        pos_out(0)
        w_weave(8, range(1, 4))
        w_widen(7)
        w_weave(6, range(4))
        w_weave(7, range(4))
        product_1(3, [2, 3])
        x_quant(4)
        w_quant(4)
        w_weave(5, range(2))
        w_exit(5)
        w_lay(11)
        product_1(4)
        x_quant(5)
        w_quant(5)
        w_weave(11, range(2))
        w_exit(11)
        product_1(5)

        w_weave(10, [0])
        w_quant(11)
        product_1(11)
        w_weave(10, range(1, 4))
        w_quant(8)
        product_1(8)
        h_add(0, [0, 1], range(2))
        pos_turn(1, 0)
        w_quant(10)
        product_1(10)
        w_weave(9, range(4))
        for u in (6, 9):
            w_quant(u)
            product_1(u, [0, 1])
        h_add(0, [0], range(2, 4))
        pos_out(1)
        h_weave(0, 0)
        w_quant(7, 4)
        product_1(7, [0, 1])
        for u in (6, 9, 7):
            product_1(u, [2])
        product_1(6, [3])

        h_gain(0, 2)
        h_add(0, [1], range(2, 4))
        h_weave(0, 1)
        h_gain(1, 2)
        h_add(1, [0], range(4))
        h_quant(0, 0)
        h_weave(1, 0, copy=nc.vector.tensor_copy)
        out_banks.extend([1, 2, 0])
        for n in range(EARLY_TILES):
            product_2(n, [0])
        h_add(1, [1], range(2))
        h_quant(1, 0)
        h_quant(0, 1)
        h_pos(0, 2, "hint10")
        h_add(1, [1], range(2, 4))
        h_weave(1, 1)
        h_gain(0, 3)
        h_weave(0, 2)
        out_banks[0:0] = [4, 5, 6]
        for n in range(COLUMN_BLOCKS):
            product_2(n, [1] if n < EARLY_TILES else range(2))
        for u in (9, 7):
            product_1(u, [3])

        issued = ready = COLUMN_BLOCKS
        for n in range(OUT_TILES):
            finish(n)
            if n == QUANTISE_AFTER[0]:
                h_quant(1, 1)
                h_pos(1, 2, "hint11")
                h_pos(0, 3, "hsum03")
                h_gain(1, 3)
                h_weave(1, 2)
                h_weave(0, 3)
            if n == QUANTISE_AFTER[1]:
                h_quant(0, 2)
                h_quant(1, 2)
                h_pos(1, 3, "hint12")
                h_weave(1, 3)
            if n == QUANTISE_AFTER[2]:
                h_quant(0, 3)
                h_quant(1, 3)
            if n in QUANTISE_AFTER:
                ready = ready + COLUMN_BLOCKS
            if n == COLUMN_BLOCKS:
                out_banks[0:0] = [7, 3]
            for m in range(issued, min(n + AHEAD, ready)):
                product_2(m)
            issued = max(issued, min(n + AHEAD, ready))
